import numpy as np, ml_dtypes
CORES = [36,164,52,180,100,228,116,244]
N = 8
import mx_ref
BF = ml_dtypes.bfloat16
def gentries(a):
    return np.ascontiguousarray(a.reshape(8, 16, -1).transpose(0, 2, 1)).reshape(8, -1)
def gtable(e):
    e = np.asarray(e); return np.ascontiguousarray(e.reshape(8, -1, 16).transpose(0, 2, 1)).reshape(128, -1).astype(np.int32)
def gcols(t, e):
    v = np.concatenate([t.reshape(8, 16, -1, 4), np.zeros((8, 16, 1, 4), BF)], axis=2)
    return np.ascontiguousarray(np.stack([v[g][:, e[g]] for g in range(8)])).reshape(128, -1)
def tile(rs):
    return np.stack(rs, axis=2).reshape(128, -1).astype(BF)
def pick(q, e):
    c = np.concatenate([q[0].reshape(128, -1, 4), np.zeros((128, 1, 4), np.uint8)], axis=1); s = np.concatenate([q[1], np.ones((16, 1), np.uint8)], axis=1)
    return (np.ascontiguousarray(c[:, e].reshape(128, -1)), np.ascontiguousarray(s[:, e]))
def join(*qs):
    return (np.concatenate([q[0] for q in qs], axis=1), np.concatenate([q[1] for q in qs], axis=1))
def put(q, e, v):
    c, s = q[0].reshape(128, -1, 4).copy(), q[1].copy(); c[:, e] = v[0].reshape(128, -1, 4); s[:, e] = v[1]
    return (c.reshape(128, -1), s)
def pk(c, s):
    return (np.ascontiguousarray(c), mx_ref.live(s))
def emit(q):
    return q[0], q[1]
def packed(v, rng):
    q = [mx_ref.quantize(np.ascontiguousarray(v[r])) for r in range(N)]
    return np.stack([a for a, b in q]), np.stack([mx_ref.plane(b, rng) for a, b in q])
def values_of_codes():
    e, c = np.zeros((128, 128, 4), np.float32), np.zeros((128, 2, 4), np.uint8)
    e[np.arange(128), np.arange(128), 0] = 1
    c[:127, :, 0] = np.arange(256).reshape(2, 128).T[:127]
    return mx_ref.matmul(mx_ref.quantize(e.reshape(128, 512).astype(BF)), (c.reshape(128, 8), np.full((16, 2), 127, np.uint8))).T.reshape(-1).astype(np.float64)
CODE_VALUE, SCALE_VALUE = values_of_codes(), 2.0 ** (np.arange(256) - 127.0)
def decode(q):
    return (CODE_VALUE[q[0]].reshape(16, 8, -1, 4) * SCALE_VALUE[q[1]][:, None, :, None] + 0.0).reshape(128, -1).astype(np.float32)
def f(rng, *shape):
    return mx_ref.flush((rng.standard_normal(shape, dtype=np.float32) * np.exp2(rng.integers(-2, 3, shape[:-1] + (1,)))).astype(BF))
def wide(rng, *shape, cols=0):
    v = rng.standard_normal(shape, dtype=np.float32) * np.exp2(rng.integers(-12, 13, shape)).astype(np.float32)
    if cols: v *= np.repeat(np.exp2(rng.integers(-cols, cols + 1, shape[:-2] + (1, shape[-1] // 4))) * (rng.random(shape[:-2] + (1, shape[-1] // 4)) > 0.0625), 4, axis=-1).astype(np.float32)
    return mx_ref.flush(v.astype(BF))
C, F = 352, 176
STEP = [2, 4, 1]
def big(v):
    v = v.astype(np.float32)
    v[np.abs(v) < np.float32(2.0 ** -16)] = 0
    return v.astype(BF)
def numbers_of(rng):
    return {"x": big(f(rng, N, 128, 4 * C)), "u": np.array(f(rng, N, 128, 512)), "v": np.array(f(rng, N, 128, 512))}
def stored(q):
    return {k: np.stack([gtable(q[i, r]) for r in range(N)]) for i, k in enumerate(("pl", "dl", "kl"))}
def lists(rng):
    return stored(rng.permuted(np.tile(np.arange(C), (3, N, 8, 1)), axis=3))
def layers(rng):
    return big(f(rng, N, 128, 2048)).reshape(N, 8, 16, 4, 8, 16, 4)
def weights(rng, w):
    c, s = packed(np.ascontiguousarray(w).reshape(N, 128, 2048), rng)
    return {"wc": c, "ws": s}
def deciding(d):
    u = d["u"].reshape(N, 8, 16, 8, 16, 4)
    u[:, :, :, :, :4] = 0
    return u
def setup_inputs(rng):
    return {**numbers_of(rng), **lists(rng), **weights(rng, layers(rng))}
def setup_inputs_ties(rng):
    d = numbers_of(rng)
    o = rng.permutation(N)
    k = rng.integers(-1, 2, (N, 8, C, 4)).astype(np.float32)
    k[o[1]] = 1
    a = np.exp2(rng.integers(-3, 4, 8).astype(np.float32))
    x = d["x"].reshape(N, 8, 16, C, 4)
    x[:, :, 0] = k.astype(BF)
    x[:, :, 4:6] = 0
    x[:, :, 4, :, 0] = 1.96875 * 2.0 ** 5
    x[:, :, 5, :, 0] = 1.125 * 2.0 ** -8
    x[:, :, 8:] = 0
    x[:, :, 8, :, 0] = (-1.125 * a)[None, :, None].astype(BF)
    x[:, :, 10, :, 0] = (-0.0703125 * a)[None, :, None].astype(BF)
    c = np.ones(N, np.float32)
    c[o[0]] = 0
    c[o[2]] = -1
    u = deciding(d)
    w = layers(rng)
    w[:] = 0
    for g in range(8):
        w[:, g, 8, 0, g, 8, 0] = -28.0
        w[:, g, 5, 0, g, 11, 0] = 4.0
        for b in range(4):
            w[:, g, 10, b, g, 9, 0] = -2.0 ** (b - 5)
            u[:, g, 0, g, b, b] = c.astype(BF)
    return {**d, **lists(rng), **weights(rng, w)}
def setup_inputs_near(rng):
    d = numbers_of(rng)
    o = rng.permutation(N) % 4
    x = d["x"].astype(np.float32).reshape(N, 8, 16, C, 4)
    x[:, :, :10] = 0
    u = deciding(d)
    w = layers(rng)
    w[:, :, :10] = 0
    w[:, :, :, :, :, :10] = 0
    for r in range(N):
        k = 2.0 ** -30 if o[r] == 0 else 1.0
        s = rng.integers(-1, 2, (8, C, 4)).astype(np.float64)
        if o[r] == 3:
            x[r] = 0
            x[r, :, 2, :, 0] = 2.0 ** -30
            x[r, :, 7, :, 0] = 2.0 ** -30
            x[r, :, 8] = rng.choice([-1.0, 1.0], (8, C, 4)) * 2.0 ** -29
            x[r, :, 9, :, 0] = 2.0 ** -29
            w[r] = 0
            for g in range(8):
                w[r, g, 7, 0, g, 2, 0] = 32.0
                for b in range(4):
                    w[r, g, 8, b, g, 0, b] = 2.0 ** -10
                    w[r, g, 8, b, g, 1, b] = -2.0 ** -10
                    w[r, g, 0, b, g, 3, b] = 128.0
                    w[r, g, 8, b, g, 5, b] = 2.0 ** -11
                    w[r, g, 0, b, g, 5, b] = 0.5
                    u[r, g, 0, g, b, b] = 1.125 * 2.0 ** -30
                    u[r, g, 1, g, b, b] = 2.0 ** -30
            continue
        if o[r] == 1:
            s *= np.exp2(rng.integers(0, 3, (8, C, 1)).astype(np.float64))
            x[r, :, 0] = 1.125 * s
            x[r, :, 1] = -s
            x[r, :, 7, :, 0] = 1.96875 * 2.0 ** 13
        else:
            x[r, :, 0] = 1.125 * s * k
            x[r, :, 1] = -1.25 * s * k
            x[r, :, 2, :, 0] = k
        for g, j in zip(rng.permutation(8)[:4], [0, C - 1, int(rng.integers(C)), int(rng.integers(C))]): x[r, g, 0, j, 0] = 2.0 ** 30 * rng.choice([-1.0, 1.0])
        for g in range(8):
            for b in range(4):
                u[r, g, 0, g, b, b] = 1.0 if o[r] == 1 else 1.125 * k
                u[r, g, 1, g, b, b] = k
    d["x"] = x.reshape(N, 128, 4 * C).astype(BF)
    return {**d, **lists(rng), **weights(rng, w)}
def setup_inputs_late(rng):
    d = numbers_of(rng)
    o = rng.permutation(N) % 4
    e = np.stack([o & 1, o >> 1, (o + 1) & 1, ((o + 1) >> 1) & 1], axis=1) * 2.0 - 1.0
    d["x"].reshape(N, 8, 16, C, 4)[:, :, 0] = e[:, None, None, :].astype(np.float32).astype(BF)
    u = deciding(d)
    for g in range(8):
        for b in range(4): u[:, g, 0, g, b, b] = 1
    w = layers(rng)
    w[:, :, :, :, :, 0] = (w[:, :, :, :, :, 0].astype(np.float32) * 4).astype(BF)
    return {**d, **lists(rng), **weights(rng, w)}
def setup_inputs_ends(rng):
    d = numbers_of(rng)
    o, e = rng.permutation(N) % 4, rng.permutation(N) % 4
    s = rng.choice([-1.0, 1.0], (N, 128, C, 4))
    s[o == 0] = -1
    s[o == 1] = rng.choice([-1.0, 1.0], (N, 1, C, 1))[o == 1]
    x = s * (0.76 + 0.02 * rng.random((N, 128, C, 4))) * 2.0 ** 30
    x[o == 3] = 2.0 ** -30
    size = np.where(o == 3, 2.0 ** -30, 2.0 ** 30)
    k = np.stack([rng.permutation(8) for r in range(N)])
    a = np.stack([k & 1, (k >> 1) & 1, k >> 2, (k ^ (k >> 1)) & 1], axis=2) * 2.0 - 1.0
    a[k < 2] = 0
    a = a * size[:, None, None]
    deciding(d)[:, :, :, :, :4] = a.astype(np.float32).astype(BF)[:, None, None, :, :, None]
    v = rng.choice([-1.0, 1.0], (N, 128, 512)) * size[:, None, None]
    q = rng.integers(0, C, (3, N, 8, C))
    q[:, e == 0] = C - 1
    q[:, e == 1] = 0
    q[:, e == 1, 7] = C - 1
    q[:, e == 2] = rng.integers(0, 2, (3, 1, 8, C)) * (C - 1)
    w = np.zeros((N, 128, 4, 128, 4), np.float32)
    i = np.arange(128)
    for b in range(4): w[:, i, b, i, b] = np.where(o[:, None] == 3, 128.0, np.where((i >> 4) % 2 == 0, -0.25, 2.0 ** -12)[None, :])
    d["x"] = x.astype(np.float32).reshape(N, 128, 4 * C).astype(BF)
    d["v"] = v.astype(np.float32).astype(BF)
    return {**d, **stored(q), **weights(rng, w.astype(BF))}
def setup_inputs_spread(rng):
    d = setup_inputs(rng)
    d["x"] = big(wide(rng, N, 128, 4 * C, cols=6))
    return d
def check_inputs(d):
    b = []
    for k in ("x", "u", "v"):
        a = np.abs(d[k].astype(np.float32))
        if not (np.isfinite(a).all() and ((a == 0) | (a >= 2.0 ** -30) & (a <= 2.0 ** 30)).all()): b.append("a value of " + k)
    for k in ("pl", "dl", "kl"):
        if not ((d[k] >= 0) & (d[k] < C)).all(): b.append("an entry of " + k)
    none, least, most = [emit(mx_ref.quantize(np.full((128, 16), k, np.float32).astype(BF)))[1][0, 0] for k in (0.0, 2.0 ** -12, 2.0 ** 7)]
    for r in range(N):
        if ((d["wc"][r] == 0x7F) | (d["wc"][r] == 0xFF)).any(): b.append("wc: a code that is no number")
        s = mx_ref.live(d["ws"][r])
        if ((s != none) & ((s < least) | (s > most))).any(): b.append("ws: a scale out of range")
        if (((d["wc"][r].reshape(16, 8, 512, 4) & 0x7F) != 0) & (s == none)[:, None, :, None]).any(): b.append("wc: a code other than zero under the scale of zeros")
    return b
def at(a, e):
    return np.take_along_axis(a, e, axis=1)
def reference(x, u, v, pl, dl, kl, wc, ws):
    qu = [mx_ref.quantize(u[r]) for r in range(N)]
    lay = [pk(wc[r], ws[r]) for r in range(N)]
    drawn = [np.stack([gentries(pl[r]), gentries(dl[r]), gentries(kl[r])]).astype(np.int64) for r in range(N)]
    link = [drawn[r] for r in range(N)]
    now = [x[r] for r in range(N)]
    for step in STEP:
        made = []
        for r in range(N):
            bit = mx_ref.matmul(qu[r], mx_ref.quantize(now[r])).reshape(8, 16, C) > 0
            for j in range(2):
                p, d, k = link[r]
                one, two = at(bit[:, 2 * j], p), at(bit[:, 2 * j + 1], p)
                t = np.where(two, at(p, p), at(d, p))
                there = np.stack([at(p, t), at(d, t), at(k, t)])
                link[r] = np.where(one, there, np.where(two, drawn[r], np.stack([d, k, p])))
            p, d, k = link[r]
            z = ((gcols(now[r], p).astype(np.float32) + gcols(now[r], k).astype(np.float32)) * np.float32(0.5)).astype(BF)
            q = mx_ref.quantize(z)
            made.append(tile([mx_ref.matmul(pick(lay[r], np.arange(128 * b, 128 * b + 128)), q) * np.float32(0.03125) for b in range(4)]))
        new = []
        for r in range(N):
            i = (r - step) % N
            m = at(link[i][2], link[r][0])
            far = gcols(decode(mx_ref.quantize(made[i])).astype(BF), m[:, :F])
            own = gcols(made[r], m[:, F:])
            new.append((now[r].astype(np.float32) + np.concatenate([far, own], axis=1).astype(np.float32)).astype(BF))
        now = new
    y, lk = np.zeros((N, 128, C), np.float32), np.zeros((N, 8, 3 * C), np.float32)
    oc, osc = np.zeros((N, 128, 4 * C), np.uint8), np.zeros((N, 16, C), np.uint8)
    for r in range(N):
        q = mx_ref.quantize(now[r])
        y[r] = mx_ref.matmul(mx_ref.quantize(v[r]), q)
        lk[r] = np.concatenate([link[r][0], link[r][1], link[r][2]], axis=1)
        oc[r], osc[r] = emit(q)
    return {"y": y, "lk": lk, "oc": oc, "osc": osc}

@@ -1,0 +1,511 @@
+from concourse.mybir import dt, AluOpType as AO, ActivationFunctionType as AF
+
+C, F = 352, 176
+STEP = [2, 4, 1]
+MID = 176
+ROT, DRAWN = 368, 720
+B16, F32, I32, U16, U8, MXC = "bfloat16", "float32", "int32", "uint16", "uint8", "float8_e4m3fn_x4"
+
+SCRATCH = {
+    "tbi": ("sbuf", [128, 96], I32), "tbs": ("sbuf", [128, 256], B16), "ttb": ("sbuf", [128, 128], B16), "tf": ("sbuf", [128, 368], B16),
+    "ones": ("sbuf", [128, 512], B16), "eb": ("sbuf", [128, 2048], B16), "qe": ("sbuf", [128, 512], MXC), "se": ("sbuf", [128, 512], U8),
+    "ci": ("sbuf", [128, 16], I32), "cf": ("sbuf", [128, 64], F32), "rc": ("sbuf", [128, 40], F32), "lc": ("sbuf", [128, 32], F32),
+    "i2": ("sbuf", [128, 24], F32), "gam": ("sbuf", [128, 48], F32), "offi": ("sbuf", [128, 24], U16), "pk": ("sbuf", [128, 16], U16),
+    "wq": ("sbuf", [128, 512], MXC), "wp": ("sbuf", [128, 512], U8),
+    "ut": ("sbuf", [128, 512], B16), "qu": ("sbuf", [128, 128], MXC), "su": ("sbuf", [128, 128], U8),
+    "vt": ("sbuf", [128, 512], B16), "qv": ("sbuf", [128, 128], MXC), "sv": ("sbuf", [128, 128], U8),
+    "x0": ("sbuf", [128, 4 * C], B16), "x1": ("sbuf", [128, 4 * C], B16), "x2": ("sbuf", [128, 4 * C], B16), "x3": ("sbuf", [128, 4 * C], B16),
+    "xp": ("sbuf", [128, 4 * C], B16), "hp": ("sbuf", [128, 4 * C], B16), "zp": ("sbuf", [128, 4 * C], B16), "zt": ("sbuf", [128, 4 * C], B16),
+    "ft": ("sbuf", [128, 4 * F], B16),
+    "qx": ("sbuf", [128, C], MXC), "sx": ("sbuf", [128, C], U8), "qz": ("sbuf", [128, C], MXC), "sz": ("sbuf", [128, C], U8),
+    "bt": ("sbuf", [128, C], B16), "wr": ("sbuf", [128, 1408], B16), "td": ("sbuf", [128, 32], U16), "tp": ("sbuf", [128, 32], U16), "wa": ("sbuf", [128, 1792], B16), "wb": ("sbuf", [128, 1088], B16),
+    "gb": ("sbuf", [128, 384], B16), "gl": ("sbuf", [128, 384], B16), "mf": ("sbuf", [128, 384], B16), "mo": ("sbuf", [128, 384], B16),
+    "gt": ("sbuf", [128, 752], B16), "glt": ("sbuf", [128, 752], B16), "n1": ("sbuf", [128, 752], B16), "n2": ("sbuf", [128, 752], B16),
+    "kr": ("sbuf", [128, C], B16), "sm": ("sbuf", [128, 480], F32),
+    "o1": ("sbuf", [128, 32], U16), "o2": ("sbuf", [128, 32], U16), "op1": ("sbuf", [128, 32], U16), "ok": ("sbuf", [128, 32], U16),
+    "opi": ("sbuf", [128, 32], U16), "om": ("sbuf", [128, 16], U16), "oo": ("sbuf", [128, 16], U16),
+    "lkt": ("sbuf", [128, C], F32), "yt": ("sbuf", [128, C], F32),
+    "ps": ("psum", [128, 4096], F32),
+}
+for _r in range(3):
+    SCRATCH["opn%d" % _r] = ("sbuf", [128, 32], U16)
+    SCRATCH["ks%d" % _r] = ("sbuf", [128, 22], B16)
+    SCRATCH["pin%d" % _r] = ("sbuf", [128, 22], U16)
+    SCRATCH["kin%d" % _r] = ("sbuf", [128, 22], B16)
+    SCRATCH["qf%d" % _r] = ("sbuf", [128, F], MXC)
+    SCRATCH["sf%d" % _r] = ("sbuf", [128, F], U8)
+    SCRATCH["qin%d" % _r] = ("sbuf", [128, F], MXC)
+    SCRATCH["sin%d" % _r] = ("sbuf", [128, F], U8)
+SEMAPHORES = ["cv", "cs", "ct", "cg", "sent", "sty", "sta",
+              "ldp", "ldd", "ldk", "ldx0", "ldx1", "ldu", "ldv", "ldwc", "ldws"]
+SEMAPHORES += [k + str(r) for r in range(3) for k in ("ap", "ak", "ac", "as")]
+
+
+def make_tracker(g, T):
+    queues = {"v": g.vector, "s": g.scalar, "t": g.tensor, "g": g, "y": g.sync}
+    own = {"v": "cv", "s": "cs", "t": "ct", "g": "cg"}
+    count = {}
+    known = {q: {} for q in queues}
+    snaps = {}
+    hist = {}
+
+    def span(r):
+        n, lo, hi, st = r
+        return (n, lo // 512 * 512, (hi + 511) // 512 * 512, 1) if n == "ps" else r
+
+    def meet(a, b):
+        if a[1] >= b[2] or b[1] >= a[2]:
+            return False
+        return not (a[3] == b[3] and a[3] > 1 and (a[1] - b[1]) % a[3])
+
+    def note(r, write, tok):
+        r = span(r)
+        h = hist.setdefault(r[0], [])
+        if write and r[3] == 1:
+            h[:] = [e for e in h if not (r[1] <= e[0][1] and e[0][2] <= r[2])]
+        h.append((r, write, tok))
+
+    def wait(q, need):
+        for sem in sorted(need):
+            val = need[sem]
+            if known[q].get(sem, 0) >= val:
+                continue
+            if any(o != sem and known[q].get(o, 0) < need[o] and snaps.get((o, need[o]), {}).get(sem, 0) >= val for o in need):
+                continue
+            queues[q].wait_ge(T.sem[sem], val)
+        for sem in need:
+            known[q][sem] = max(known[q].get(sem, 0), need[sem])
+            for s, v in snaps.get((sem, need[sem]), {}).items():
+                known[q][s] = max(known[q].get(s, 0), v)
+
+    def deps(reads, writes):
+        need = {}
+        for rs, w in ((reads, False), (writes, True)):
+            for r in rs:
+                r = span(r)
+                for e, ew, tok in hist.get(r[0], []):
+                    if (w or ew) and meet(r, e):
+                        need[tok[0]] = max(need.get(tok[0], 0), tok[1])
+        return need
+
+    def emit(q, call, reads, writes, sem=None, inc=1):
+        wait(q, deps(reads, writes))
+        name = sem or own[q]
+        call().then_inc(T.sem[name], inc)
+        count[name] = count.get(name, 0) + inc
+        tok = (name, count[name])
+        snaps[tok] = dict(known[q])
+        for r in reads:
+            note(r, False, tok)
+        for r in writes:
+            note(r, True, tok)
+
+    def arrive(r, sem, val):
+        note(r, True, (sem, val))
+
+    def ready(q, reads):
+        wait(q, deps(reads, []))
+
+    return emit, arrive, ready, count
+
+
+def rank_program(g, core, T, topo):
+    rank = T.rank_of(core)
+    if rank is None:
+        return
+    emit, arrive, ready, count = make_tracker(g, T)
+    V, S, PE = g.vector, g.scalar, g.tensor
+
+    def R(n, lo, hi, st=1):
+        return (n, lo, hi, st)
+
+    def ap(r):
+        return T[r[0]][:, r[1]:r[2]] if r[3] == 1 else T[r[0]][:, r[1]:r[2]:r[3]]
+
+    def src(r, off):
+        return ap(r) if off is None else ap(r).indirect(ap(off))
+
+    def rd(*rs):
+        return [r for r in rs if isinstance(r, tuple)]
+
+    def val(x):
+        return ap(x) if isinstance(x, tuple) else x
+
+    def copy(out, in_, off=None):
+        emit("v", lambda: V.tensor_copy(ap(out), src(in_, off)), rd(in_, off), [out])
+
+    def ts(out, in_, s1, op0, s2=None, op1=None, off=None):
+        if op1 is None:
+            emit("v", lambda: V.tensor_scalar(ap(out), src(in_, off), val(s1), None, op0), rd(in_, off, s1), [out])
+        else:
+            emit("v", lambda: V.tensor_scalar(ap(out), src(in_, off), val(s1), val(s2), op0, op1), rd(in_, off, s1, s2), [out])
+
+    def tt(out, a, b, op, off=None):
+        emit("v", lambda: V.tensor_tensor(ap(out), src(a, off), ap(b), op), rd(a, b, off), [out])
+
+    def tr(out, in_):
+        emit("v", lambda: V.transpose(ap(out), ap(in_)), [in_], [out])
+
+    def ms(out, c):
+        emit("v", lambda: V.memset(ap(out), c), [], [out])
+
+    def qm(q, s, in_):
+        emit("v", lambda: V.quantize_mx(ap(q), ap(s), ap(in_)), [in_], [q, s])
+
+    def act(out, in_, off=None, scale=1.0, bias=None):
+        if bias is not None:
+            emit("s", lambda: S.activation(ap(out), src(in_, off), AF.Identity, bias=ap(bias)), rd(in_, off, bias), [out])
+            return
+        func = AF.Identity if isinstance(scale, tuple) else AF.Copy
+        emit("s", lambda: S.activation(ap(out), src(in_, off), func, scale=val(scale)), rd(in_, off, scale), [out])
+
+    def mm(bank, n, w, ws, x, xs):
+        out = R("ps", 512 * bank, 512 * bank + n)
+        emit("t", lambda: PE.matmul_mx(ap(out), ap(w), ap(ws), ap(x), ap(xs), True, True), [w, ws, x, xs], [out])
+        return out
+
+    def load(q, out, in_ap, sem, code=False):
+        eng = {"y": g.sync, "s": g.scalar}[q]
+        emit(q, lambda: eng.dma_start(ap(out).bitcast(dt.uint8) if code else ap(out), in_ap), [], [out], sem, 16)
+
+    def iota(out, pattern, base, cm):
+        emit("g", lambda: g.iota(ap(out), pattern, base, cm, allow_small_or_imprecise_dtypes=True), [], [out])
+
+    load("s", R("tbi", 0, 22), T.pl[:], "ldp")
+    load("y", R("x0", 4 * F, 4 * C), T.x[:, 4 * F:4 * C], "ldx1")
+    load("s", R("tbi", 22, 44), T.dl[:], "ldd")
+    load("y", R("x0", 0, 4 * F), T.x[:, 0:4 * F], "ldx0")
+    load("s", R("tbi", 44, 66), T.kl[:], "ldk")
+    load("s", R("ut", 0, 512), T.u[:], "ldu")
+    load("y", R("wq", 0, 512), T.wc[:], "ldwc", True)
+    load("y", R("wp", 0, 512), T.ws[:], "ldws")
+    load("y", R("vt", 0, 512), T.v[:], "ldv")
+
+    ip = R("ci", 0, 1)
+    emit("g", lambda: g.iota(ap(ip), [[0, 1]], 0, 1), [], [ip])
+    iota(R("rc", 0, 5), [[0, 5]], 1000, 0)
+    iota(R("rc", 5, 17), [[0, 4], [22, 3]], 0, 0)
+    iota(R("rc", 16, 21), [[0, 5]], 1000, 0)
+    iota(R("rc", 21, 33), [[0, 4], [22, 3]], 0, 0)
+    iota(R("i2", 0, 22), [[2, 11], [0, 2]], 0, 0)
+    iota(R("gam", 0, 24), [[32, 12], [0, 2]], ROT + 176 - 16, 0)
+    iota(R("gam", 24, 46), [[32, 11], [0, 2]], ROT + 176, 0)
+    iota(R("ones", 0, 512), [[0, 512]], 1, 0)
+    for b in range(4):
+        e = R("eb", 512 * b, 512 * b + 512)
+        emit("g", lambda: g.affine_select(ap(e), ap(R("ones", 0, 512)), [[-1, 512]], AO.is_equal, 0.0, b, 4), [R("ones", 0, 512)], [e])
+    ms(R("tbs", 224, 256), 0.0)
+    ms(R("tbs", 66, 96), 0.0)
+    for n, a in (("ttb", 0), ("ttb", 112), ("tf", 352), ("gl", 0), ("gl", 368), ("wa", 0), ("wa", 368), ("wb", 0), ("wb", 368),
+                 ("gb", 0), ("gb", 368), ("n1", 736), ("n2", 736), ("mf", 0), ("mo", 368)):
+        act(R(n, a, a + 16), R("tbs", 224, 240))
+    act(R("sm", 384, 400), R("tbs", 224, 240))
+    act(R("sm", 400, 432), R("tbs", 224, 256))
+    def cf(i):
+        return R("cf", i, i + 1)
+
+    def ci(i):
+        return R("ci", i, i + 1)
+    ts(ci(1), ip, 15, AO.bitwise_and)
+    ts(ci(2), ip, 4, AO.arith_shift_right, 1, AO.bitwise_and)
+    ts(ci(3), ip, 31, AO.bitwise_and)
+    tr(R("lc", 0, 32), R("rc", 0, 32))
+    copy(R("cf", 0, 3), R("ci", 1, 4))
+    tt(ci(4), ci(1), ci(2), AO.add)
+    q_, par, i32, l32, odd = cf(0), cf(1), cf(2), R("lc", 0, 1), cf(3)
+    ts(cf(4), par, 97.0, AO.mult)
+    ts(cf(5), par, -127.0, AO.mult, 128.0, AO.add)
+    ts(ci(5), ci(4), 1, AO.bitwise_and)
+    tt(cf(6), cf(4), l32, AO.add)
+    tt(cf(7), cf(5), l32, AO.add)
+    copy(odd, ci(5))
+    ts(cf(6), cf(6), 224.0, AO.min)
+    ts(cf(7), cf(7), 224.0, AO.min)
+    ts(R("offi", 0, 22, 2), R("i2", 0, 22, 2), cf(6), AO.add)
+    ts(R("offi", 1, 22, 2), R("i2", 1, 22, 2), cf(7), AO.add)
+    RM, THR, WT, NB = cf(8), cf(9), cf(19), cf(20)
+
+    ts(R("tbs", 0, 66), R("tbi", 0, 66), float(-MID), AO.add)
+    copy(R("opi", 0, 22), R("tbi", 0, 22))
+    tr(R("ttb", 16, 112), R("tbs", 0, 96))
+    tr(R("tbs", 96, 224), R("ttb", 0, 128))
+    copy(R("tf", 0, 352), R("tbs", 0, 256), R("offi", 0, 22))
+    tr(R("wa", 16, 368), R("tf", 0, 352))
+    GAM = R("gam", 0, 46)
+
+    def sm(i):
+        return R("sm", 48 * i, 48 * i + 46)
+
+    PM, PP, PK, PK1, PO, PD = R("pk", 0, 2), R("pk", 2, 4), R("pk", 4, 6), R("pk", 4, 5), R("pk", 6, 7), R("pk", 8, 10)
+
+    def prelinks(off):
+        act(R("gl", 16, 368), R("wa", 16, 368), off)
+
+    def prelinks2():
+        tr(R("glt", 0, 384), R("gl", 0, 384))
+        tr(R("glt", 384, 736), R("gl", 16, 368))
+
+    def prelinks3():
+        for o, pick, a in (("td", PD, 1088), ("tp", PP, 1440)):
+            ts(R(o, 0, 32), R("glt", 0, 736), float(MID), AO.add, off=pick)
+            act(R("wa", a, a + C), R("wa", 16, 368), R(o, 0, 22))
+
+    def prelinks4():
+        act(R("wr", 704, 1056), R("wa", 384, 736), R("td", 0, 22))
+        act(R("wr", 1056, 1408), R("wa", 384, 736), R("tp", 0, 22))
+
+    prelinks(R("opi", 0, 22))
+    act(R("wa", 736, 1088), R("wa", 16, 368))
+    ts(cf(10), odd, -23.0, AO.mult, 24.0, AO.add)
+    ts(THR, q_, 3.5, AO.is_ge, 1e28, AO.mult)
+    ts(cf(17), q_, 0.0, AO.is_equal, 352.0, AO.mult)
+    ts(cf(18), q_, 2.0, AO.is_equal, 1696.0, AO.mult)
+    tt(cf(11), cf(10), q_, AO.add)
+    ts(WT, cf(17), cf(18), AO.add, 352.0, AO.add)
+    ts(cf(12), cf(11), 16.0, AO.add, 45.0, AO.min)
+    ts(PP, R("cf", 11, 13), 16.0, AO.mult, 5.0, AO.add)
+    ts(PD, R("cf", 11, 13), 16.0, AO.mult, 6.0, AO.add)
+    copy(PM, R("cf", 11, 13))
+    rest = [
+        lambda: ts(GAM, GAM, i32, AO.add),
+        lambda: ts(cf(21), q_, 2.0, AO.is_equal, -1024.0, AO.mult),
+        lambda: ts(cf(22), q_, 3.0, AO.is_equal, -176.0, AO.mult),
+        lambda: tt(NB, cf(21), cf(22), AO.add),
+        lambda: ts(RM, l32, 500.0, AO.is_lt),
+        lambda: ts(PK, R("cf", 11, 13), 16.0, AO.mult, 7.0, AO.add),
+        lambda: ts(cf(14), odd, 23.0, AO.mult, 12.0, AO.add),
+        lambda: ms(cf(23), float(MID)),
+        lambda: tt(cf(15), cf(14), q_, AO.add),
+        lambda: ts(cf(16), cf(15), 45.0, AO.min, 16.0, AO.mult),
+        lambda: ts(PO, cf(16), 7.0, AO.add),
+    ]
+
+    def fill(n):
+        for i in range(n):
+            if rest:
+                rest.pop(0)()
+
+    def state_half(r, h):
+        lo, hi = (0, F) if h == 0 else (F, C)
+        qm(R("qx", lo, hi), R("sx", lo, hi), R("x%d" % r, 4 * lo, 4 * hi))
+
+    def signs_mm(h):
+        lo, hi = (0, F) if h == 0 else (F, C)
+        mm(5 - h, F, R("qu", 0, 128), R("su", 0, 128), R("qx", lo, hi), R("sx", lo, hi))
+
+    def signs_ts(h):
+        lo, hi = (0, F) if h == 0 else (F, C)
+        ts(R("bt", lo, hi), R("ps", 512 * (5 - h), 512 * (5 - h) + F), THR, AO.is_gt, WT, AO.mult)
+
+    def planes(r, h):
+        lo, hi = (0, F) if h == 0 else (F, C)
+        for t in range(4):
+            act(R("xp", C * t + lo, C * t + hi), R("x%d" % r, 4 * lo + t, 4 * hi, 4), scale=0.5)
+
+    prelinks2()
+    prelinks3()
+    state_half(0, 1)
+    qm(R("qu", 0, 128), R("su", 0, 128), R("ut", 0, 512))
+    state_half(0, 0)
+    tr(R("wa", 384, 736), R("tf", 1, 353))
+    signs_mm(1)
+    signs_mm(0)
+    signs_ts(1)
+    signs_ts(0)
+
+    ALL = R("wa", 384, 1792)
+    ALLB = R("wb", 16, 1088)
+
+    def turn(dst, srcb, a, b):
+        tr(R(dst, 384 + a, 384 + b), R(srcb, 16 + a, 16 + b))
+        e = 384 if b == C else b
+        tr(R(dst, a, e), R(srcb, a, e))
+
+    dst = T.cores[0]
+    offp = R("opi", 0, 22)
+    for r in range(3):
+        s = STEP[r]
+        source, target = T.cores[(rank - s) % 8], T.cores[(rank + s) % 8]
+        last = r == 2
+        n_all = len(topo.engines(core, target))
+        PIN = R("pin%d" % r, 0, 12)
+        arrive(PIN, "ap%d" % r, len(topo.engines(source, core)))
+        arrive(R("kin%d" % r, 0, 22), "ak%d" % r, n_all)
+        arrive(R("qin%d" % r, 0, F), "ac%d" % r, n_all)
+        arrive(R("sin%d" % r, 0, F), "as%d" % r, n_all)
+        X, XN = "x%d" % r, "x%d" % (r + 1)
+
+        k = 10
+        a = 16 * k
+        BT = R("bt", 0, C)
+        copy(R("gb", 16, 16 + a), BT, R(offp[0], 0, k))
+        act(R("gb", 16 + a, 368), BT, R(offp[0], k, 22))
+        turn("gt", "gb", 0, a)
+        turn("gt", "gb", a, C)
+        A0, A1 = R("gt", 0, 736, 16), R("gt", 1, 736, 16)
+        tt(sm(3), A0, A1, AO.add)
+        fill(1)
+        tt(sm(8), sm(3), GAM, AO.add)
+        fill(1)
+        ts(R("o1", 0, 32), R("sm", 48 * 8, 48 * 9), float(-ROT - 176), AO.add, off=PM)
+        fill(1)
+        tt(R("wb", 16, 368), ALL, BT, AO.add, off=R("o1", 0, 22))
+        if r == 0:
+            act(R("wb", 736, 1088), R("wa", 736, 1088))
+            planes(0, 1)
+        else:
+            act(R("wb", 384, 736), R("wr", 0, 1408), R("o1", 0, 22))
+        planes(r, 0)
+        fill(1)
+        turn("n1", "wb", 0, C)
+        fill(1)
+        ts(R("op1", 0, 32), R("n1", 0, 736), float(MID), AO.add, off=PP)
+        fill(1)
+
+        k = 8 if r == 0 else 10
+        a = 16 * k
+        CB = R("wb", 16, 368)
+        act(R("gb", 16 + a, 368), CB, R("op1", k, 22), bias=NB)
+        ts(R("gb", 16, 16 + a), CB, NB, AO.add, off=R("op1", 0, k))
+        turn("gt", "gb", 0, a)
+        if r == 0:
+            tr(R("wb", 384, 736), R("n1", 385, 737))
+        turn("gt", "gb", a, C)
+        A2, A3, GP, GD = R("gt", 2, 736, 16), R("gt", 3, 736, 16), R("gt", 5, 736, 16), R("gt", 6, 736, 16)
+        tt(sm(1), GP, A3, AO.add)
+        tt(sm(2), GD, A3, AO.subtract)
+        tt(sm(3), GAM, A3, AO.add)
+        tt(sm(4), sm(1), sm(2), AO.max)
+        tt(sm(5), sm(3), A2, AO.subtract)
+        tt(sm(6), sm(4), A2, AO.add)
+        fill(1)
+        tt(sm(8), sm(6), sm(5), AO.max)
+        fill(1)
+        ts(R("o2", 0, 32), R("sm", 48 * 8, 48 * 9), -1024.0, AO.add, off=PM)
+        fill(1)
+        k = 10
+        a = 16 * k
+        act(R("wa", 16 + a, 368), ALLB, R("o2", k, 22), scale=RM)
+        ts(R("wa", 16, 16 + a), ALLB, RM, AO.mult, off=R("o2", 0, k))
+        turn("n2", "wa", 0, a)
+        turn("n2", "wa", a, C)
+        fill(1)
+        OP = "opn%d" % r
+        N2 = R("n2", 0, 736)
+        ts(R(OP, 0, 32), N2, float(MID), AO.add, off=PP)
+        KS = R("ks%d" % r, 0, 22)
+        copy(KS, R("n2", 384 + 7, 736, 16))
+        ts(R("ok", 0, 32), N2, float(MID), AO.add, off=PK)
+        offp = R(OP, 0, 22)
+
+        for d, sr, ds, sem in ((source, R(OP, 0, 12), PIN, "ap%d" % r), (target, KS, R("kin%d" % r, 0, 22), "ak%d" % r)):
+            ready("g", [sr])
+            rid, pid = topo.addr(d, core)
+            g.remote_dma(ap(ds), ap(sr), T.sem[sem], T.sem["sent"], pid, rid, topo.mask(core, d))
+            count["sent"] = count.get("sent", 0) + len(topo.engines(core, d))
+
+        if not last:
+            tr(R("wa", 384, 736), R("n2", 385, 737))
+        fill(20)
+        for c, (k0, k1) in enumerate(((0, 12), (12, 22))):
+            lo, hi = 16 * k0, 16 * k1
+            for t in range(4):
+                win = R("xp", C * t, C * t + C)
+                zp = R("zp", C * t + lo, C * t + hi)
+                act(zp, win, R(OP, k0, k1))
+                tt(R("zt", 4 * lo + t, 4 * hi, 4), win, zp, AO.add, off=R("ok", k0, k1))
+            qm(R("qz", lo, hi), R("sz", lo, hi), R("zt", 4 * lo, 4 * hi))
+            for b in range(4):
+                mm(4 * c + b, hi - lo, R("wq", 128 * b, 128 * b + 128), R("wp", 128 * b, 128 * b + 128), R("qz", lo, hi), R("sz", lo, hi))
+
+        def evict(c, b):
+            lo, w = (0, 192) if c == 0 else (192, 160)
+            bank = 512 * (4 * c + b)
+            act(R("hp", C * b + lo, C * b + lo + w), R("ps", bank, bank + w), scale=0.03125)
+
+        for b in range(3):
+            evict(0, b)
+        act(R("mf", 16, 208), R("wa", 16, 368), R("pin%d" % r, 0, 12))
+        evict(0, 3)
+        if r == 0:
+            for b in range(4):
+                qm(R("qe", 128 * b, 128 * b + 128), R("se", 128 * b, 128 * b + 128), R("eb", 512 * b, 512 * b + 512))
+        if r == 1:
+            qm(R("qv", 0, 128), R("sv", 0, 128), R("vt", 0, 512))
+        turn("gt", "mf", 0, 192)
+        ts(R("om", 0, 16), R("gt", 0, 736), float(MID), AO.add, off=PK1)
+        for b in range(4):
+            evict(1, b)
+            ft = R("ft", b, 4 * F, 4)
+            hw = R("hp", C * b, C * b + C)
+            if b < 3:
+                copy(ft, hw, R("om", 0, 11))
+            else:
+                act(ft, hw, R("om", 0, 11))
+        qm(R("qf%d" % r, 0, F), R("sf%d" % r, 0, F), R("ft", 0, 4 * F))
+
+        QF, SF = R("qf%d" % r, 0, F), R("sf%d" % r, 0, F)
+        ready("g", [QF, SF])
+        rid, pid = topo.addr(target, core)
+        m = topo.mask(core, target)
+        g.remote_dma(ap(R("qin%d" % r, 0, F)).bitcast(dt.uint8), ap(QF).bitcast(dt.uint8), T.sem["ac%d" % r], T.sem["sent"], pid, rid, m)
+        g.remote_dma(ap(R("sin%d" % r, 0, F)), ap(SF), T.sem["as%d" % r], T.sem["sent"], pid, rid, m)
+        count["sent"] += 2 * n_all
+
+        if not last:
+            prelinks(offp)
+        copy(R("n1", 384 + 7, 736, 16), R("kin%d" % r, 0, 22))
+        tr(R("kr", 0, C), R("n1", 384, 736))
+        act(R("mo", 176, 368), R("kr", 0, C), R(OP, 10, 22))
+        if not last:
+            prelinks2()
+            prelinks3()
+        tr(R("gt", 384 + 160, 736), R("mo", 176, 368))
+        tr(R("gt", 192, 384), R("mo", 192, 384))
+        ts(R("oo", 0, 16), R("gt", 0, 736), float(MID), AO.add, off=PO)
+        for t in range(4):
+            tt(R(XN, 4 * F + t, 4 * C, 4), R("hp", C * t, C * t + C), R(X, 4 * F + t, 4 * C, 4), AO.add, off=R("oo", 0, 11))
+        state_half(r + 1, 1)
+        if not last:
+            planes(r + 1, 1)
+            prelinks4()
+            signs_mm(1)
+            tr(R("wr", 0, 352), R("n2", 386, 738))
+            if r == 0:
+                tr(R("wr", 352, 704), R("tf", 1, 353))
+        else:
+            store(g, T, emit, ap, R, mm, act, ts, 1)
+            lkt = R("lkt", 0, C)
+            act(lkt, R("wa", 16, 368), bias=cf(23))
+            for gr in range(8):
+                emit("y", lambda: g.sync.dma_start(T.lk[gr:gr + 1, :], T.lkt[16 * gr + 5:16 * gr + 8, :]), [lkt], [], "sty", 16)
+
+        for b in range(4):
+            out = mm(b, F, R("qe", 128 * b, 128 * b + 128), R("se", 128 * b, 128 * b + 128), R("qin%d" % r, 0, F), R("sin%d" % r, 0, F))
+            tt(R(XN, b, 4 * F, 4), out, R(X, b, 4 * F, 4), AO.add)
+        state_half(r + 1, 0)
+        if not last:
+            signs_ts(1)
+            signs_mm(0)
+            signs_ts(0)
+        else:
+            store(g, T, emit, ap, R, mm, act, ts, 0)
+
+    for n in ("cv", "cs", "ct", "cg", "sent", "sty", "sta"):
+        if count.get(n):
+            g.wait_ge(T.sem[n], count[n])
+
+
+def store(g, T, emit, ap, R, mm, act, ts, h):
+    lo, hi = (0, F) if h == 0 else (F, C)
+    Q, P, Y = R("qx", lo, hi), R("sx", lo, hi), R("yt", lo, hi)
+    out = mm(5 - h, F, R("qv", 0, 128), R("sv", 0, 128), Q, P)
+    emit("y", lambda: g.sync.dma_start(T.oc[:, 4 * lo:4 * hi], ap(Q).bitcast(dt.uint8)), [Q], [], "sty", 16)
+    for k in range(4):
+        q, e, sem = ("s", g.scalar, "sta") if k % 2 else ("y", g.sync, "sty")
+        emit(q, lambda: e.dma_start(T.osc[4 * k:4 * k + 4, lo:hi], T.sx[32 * k:32 * k + 4, lo:hi]), [P], [], sem, 16)
+    if h:
+        act(Y, out)
+    else:
+        ts(Y, out, 1.0, AO.mult)
+    emit("y", lambda: g.sync.dma_start(T.y[:, lo:hi], ap(Y)), [Y], [], "sty", 16)

@@ -4,26 +4,33 @@ C, F = 352, 176
 STEP = [2, 4, 1]
 MID = 176
 ROT, DRAWN = 368, 720
+QP, QK, QD = 7, 9, 11
+LOW = -4096
 B16, F32, I32, U16, U8, MXC = "bfloat16", "float32", "int32", "uint16", "uint8", "float8_e4m3fn_x4"
 
 SCRATCH = {
-    "tbi": ("sbuf", [128, 96], I32), "tbs": ("sbuf", [128, 256], B16), "ttb": ("sbuf", [128, 128], B16), "tf": ("sbuf", [128, 368], B16),
+    "tbi": ("sbuf", [128, 96], I32), "tbs": ("sbuf", [128, 256], B16), "ttb": ("sbuf", [128, 128], B16), "tf": ("sbuf", [128, 384], B16),
     "ones": ("sbuf", [128, 512], B16), "eb": ("sbuf", [128, 2048], B16), "qe": ("sbuf", [128, 512], MXC), "se": ("sbuf", [128, 512], U8),
-    "ci": ("sbuf", [128, 16], I32), "cf": ("sbuf", [128, 64], F32), "rc": ("sbuf", [128, 40], F32), "lc": ("sbuf", [128, 32], F32),
-    "i2": ("sbuf", [128, 24], F32), "gam": ("sbuf", [128, 48], F32), "offi": ("sbuf", [128, 24], U16), "pk": ("sbuf", [128, 16], U16),
+    "ci": ("sbuf", [128, 16], I32), "cf": ("sbuf", [128, 64], F32), "rc": ("sbuf", [128, 72], F32), "lc": ("sbuf", [128, 64], F32),
+    "tb": ("sbuf", [128, 160], F32), "tc": ("sbuf", [128, 160], F32),
+    "i2": ("sbuf", [128, 32], F32), "gam": ("sbuf", [128, 48], F32), "gab": ("sbuf", [128, 48], B16),
+    "offi": ("sbuf", [128, 24], U16), "pk": ("sbuf", [128, 16], U16), "upk": ("sbuf", [128, 8], U16),
     "wq": ("sbuf", [128, 512], MXC), "wp": ("sbuf", [128, 512], U8),
     "ut": ("sbuf", [128, 512], B16), "qu": ("sbuf", [128, 128], MXC), "su": ("sbuf", [128, 128], U8),
+    "qd": ("sbuf", [128, 128], MXC), "sd": ("sbuf", [128, 128], U8),
     "vt": ("sbuf", [128, 512], B16), "qv": ("sbuf", [128, 128], MXC), "sv": ("sbuf", [128, 128], U8),
     "x0": ("sbuf", [128, 4 * C], B16), "x1": ("sbuf", [128, 4 * C], B16), "x2": ("sbuf", [128, 4 * C], B16), "x3": ("sbuf", [128, 4 * C], B16),
     "xp": ("sbuf", [128, 4 * C], B16), "hp": ("sbuf", [128, 4 * C], B16), "zp": ("sbuf", [128, 4 * C], B16), "zt": ("sbuf", [128, 4 * C], B16),
     "ft": ("sbuf", [128, 4 * F], B16),
     "qx": ("sbuf", [128, C], MXC), "sx": ("sbuf", [128, C], U8), "qz": ("sbuf", [128, C], MXC), "sz": ("sbuf", [128, C], U8),
-    "bt": ("sbuf", [128, C], B16), "wr": ("sbuf", [128, 1408], B16), "td": ("sbuf", [128, 32], U16), "tp": ("sbuf", [128, 32], U16), "wa": ("sbuf", [128, 1792], B16), "wb": ("sbuf", [128, 1088], B16),
+    "bt": ("sbuf", [128, C], B16), "wr": ("sbuf", [128, 1408], B16), "td": ("sbuf", [128, 32], U16), "tp": ("sbuf", [128, 32], U16),
+    "wa": ("sbuf", [128, 1792], B16), "wb": ("sbuf", [128, 1088], B16),
+    "gm": ("sbuf", [128, C], B16), "g1": ("sbuf", [128, C], B16), "so": ("sbuf", [128, F], B16), "s1": ("sbuf", [128, F], B16),
     "gb": ("sbuf", [128, 384], B16), "gl": ("sbuf", [128, 384], B16), "mf": ("sbuf", [128, 384], B16), "mo": ("sbuf", [128, 384], B16),
     "gt": ("sbuf", [128, 752], B16), "glt": ("sbuf", [128, 752], B16), "n1": ("sbuf", [128, 752], B16), "n2": ("sbuf", [128, 752], B16),
-    "kr": ("sbuf", [128, C], B16), "sm": ("sbuf", [128, 480], F32),
+    "mt": ("sbuf", [128, 752], B16), "kr": ("sbuf", [128, C], B16), "s2": ("sbuf", [128, 184], F32),
     "o1": ("sbuf", [128, 32], U16), "o2": ("sbuf", [128, 32], U16), "op1": ("sbuf", [128, 32], U16), "ok": ("sbuf", [128, 32], U16),
-    "opi": ("sbuf", [128, 32], U16), "om": ("sbuf", [128, 16], U16), "oo": ("sbuf", [128, 16], U16),
+    "opi": ("sbuf", [128, 32], U16), "opm": ("sbuf", [128, 32], U16), "om": ("sbuf", [128, 16], U16), "oo": ("sbuf", [128, 16], U16),
     "lkt": ("sbuf", [128, C], F32), "yt": ("sbuf", [128, C], F32),
     "ps": ("psum", [128, 4096], F32),
 }
@@ -56,7 +63,8 @@ def make_tracker(g, T):
     def meet(a, b):
         if a[1] >= b[2] or b[1] >= a[2]:
             return False
-        return not (a[3] == b[3] and a[3] > 1 and (a[1] - b[1]) % a[3])
+        st = min(a[3], b[3])
+        return not (st > 1 and a[3] % st == 0 and b[3] % st == 0 and (a[1] - b[1]) % st)
 
     def note(r, write, tok):
         r = span(r)
@@ -143,6 +151,9 @@ def rank_program(g, core, T, topo):
     def tt(out, a, b, op, off=None):
         emit("v", lambda: V.tensor_tensor(ap(out), src(a, off), ap(b), op), rd(a, b, off), [out])
 
+    def scan(out, a, b):
+        emit("v", lambda: V.tensor_tensor_scan(ap(out), ap(a), ap(b), 0.0, AO.add, AO.max), [a, b], [out])
+
     def tr(out, in_):
         emit("v", lambda: V.transpose(ap(out), ap(in_)), [in_], [out])
 
@@ -154,10 +165,17 @@ def rank_program(g, core, T, topo):
 
     def act(out, in_, off=None, scale=1.0, bias=None):
         if bias is not None:
-            emit("s", lambda: S.activation(ap(out), src(in_, off), AF.Identity, bias=ap(bias)), rd(in_, off, bias), [out])
+            emit("s", lambda: S.activation(ap(out), src(in_, off), AF.Identity, bias=val(bias), scale=val(scale)), rd(in_, off, bias, scale), [out])
+            return
+        if scale == 1.0:
+            emit("s", lambda: S.activation(ap(out), src(in_, off), AF.Copy), rd(in_, off), [out])
             return
         func = AF.Identity if isinstance(scale, tuple) else AF.Copy
         emit("s", lambda: S.activation(ap(out), src(in_, off), func, scale=val(scale)), rd(in_, off, scale), [out])
+
+    def both(out, lo, win, off, k, n=22):
+        copy(R(out, lo, lo + 16 * k), win, R(off, 0, k))
+        act(R(out, lo + 16 * k, lo + 16 * n), win, R(off, k, n))
 
     def mm(bank, n, w, ws, x, xs):
         out = R("ps", 512 * bank, 512 * bank + n)
@@ -168,39 +186,51 @@ def rank_program(g, core, T, topo):
         eng = {"y": g.sync, "s": g.scalar}[q]
         emit(q, lambda: eng.dma_start(ap(out).bitcast(dt.uint8) if code else ap(out), in_ap), [], [out], sem, 16)
 
-    def iota(out, pattern, base, cm):
+    def iota(out, pattern, base, cm=0):
         emit("g", lambda: g.iota(ap(out), pattern, base, cm, allow_small_or_imprecise_dtypes=True), [], [out])
 
     load("s", R("tbi", 0, 22), T.pl[:], "ldp")
-    load("y", R("x0", 4 * F, 4 * C), T.x[:, 4 * F:4 * C], "ldx1")
-    load("s", R("tbi", 22, 44), T.dl[:], "ldd")
+    load("y", R("tbi", 22, 44), T.kl[:], "ldk")
+    load("s", R("tbi", 44, 66), T.dl[:], "ldd")
+    load("y", R("ut", 0, 512), T.u[:], "ldu")
+    load("s", R("x0", 4 * F, 4 * C), T.x[:, 4 * F:4 * C], "ldx1")
     load("y", R("x0", 0, 4 * F), T.x[:, 0:4 * F], "ldx0")
-    load("s", R("tbi", 44, 66), T.kl[:], "ldk")
-    load("s", R("ut", 0, 512), T.u[:], "ldu")
+
+    ip = R("ci", 0, 1)
+    emit("g", lambda: g.iota(ap(ip), [[0, 1]], 0, 1), [], [ip])
+    iota(R("rc", 0, 32, 2), [[0, 16]], 1000)
+    iota(R("rc", 1, 19, 2), [[0, 3], [22, 3]], 0)
+    iota(R("rc", 17, 35, 2), [[0, 3], [22, 3]], 0)
+    iota(R("i2", 0, 22), [[2, 11], [0, 2]], 0)
+    iota(R("rc", 32, 64), [[0, 32]], 3)
+    iota(R("rc", 36, 64, 16), [[0, 2]], 2)
+    iota(R("rc", 34, 64, 8), [[0, 2], [16, 2]], 1)
+    iota(R("rc", 38, 64, 8), [[0, 2], [16, 2]], 0)
+    iota(R("i2", 24, 32), [[16, 8]], 0)
+    ms(R("tb", 0, 160), 0.0)
+    ms(R("tbs", 224, 256), 0.0)
+    ms(R("tbs", 66, 96), 0.0)
+    ms(R("so", 0, F), 2.0 * LOW)
+    iota(R("so", 0, F, 4), [[16, 22], [0, 2]], 0)
+    iota(R("gam", 0, 24), [[32, 12], [0, 2]], -16 - MID)
+    iota(R("gam", 24, 46), [[32, 11], [0, 2]], -MID)
+    iota(R("ones", 0, 512), [[0, 512]], 1)
+    for b in range(4):
+        e = R("eb", 512 * b, 512 * b + 512)
+        emit("g", lambda: g.affine_select(ap(e), ap(R("ones", 0, 512)), [[-1, 512]], AO.is_equal, 0.0, b, 4), [R("ones", 0, 512)], [e])
+    WT, KEEP, START, NB, RM = [R("tc", 32 * i, 32 * i + 1) for i in range(5)]
+    zero = R("tbs", 224, 240)
+    for i, q, st, c in ((0, 2, 8, 352), (0, 6, 8, 704), (0, 4, 16, LOW), (0, 8, 16, 704), (0, 12, 16, -352), (1, 2, 4, 1), (2, 0, 8, LOW), (4, 1, 2, 1)):
+        ms(R("tb", 32 * i + q, 32 * i + 32, st), float(c))
+    for q, c in ((0, LOW), (4, DRAWN), (8, -352), (15, LOW)):
+        act(R("tb", 96 + q, 128, 16), R("tbs", 224, 226), bias=float(c))
+    for n, a in (("ttb", 0), ("ttb", 112), ("tf", 0), ("gl", 0), ("gl", 368), ("wa", 0), ("wa", 368), ("wb", 0), ("wb", 368),
+                 ("gb", 0), ("gb", 368), ("mf", 0), ("mo", 368)):
+        act(R(n, a, a + 16), zero)
     load("y", R("wq", 0, 512), T.wc[:], "ldwc", True)
     load("y", R("wp", 0, 512), T.ws[:], "ldws")
     load("y", R("vt", 0, 512), T.v[:], "ldv")
 
-    ip = R("ci", 0, 1)
-    emit("g", lambda: g.iota(ap(ip), [[0, 1]], 0, 1), [], [ip])
-    iota(R("rc", 0, 5), [[0, 5]], 1000, 0)
-    iota(R("rc", 5, 17), [[0, 4], [22, 3]], 0, 0)
-    iota(R("rc", 16, 21), [[0, 5]], 1000, 0)
-    iota(R("rc", 21, 33), [[0, 4], [22, 3]], 0, 0)
-    iota(R("i2", 0, 22), [[2, 11], [0, 2]], 0, 0)
-    iota(R("gam", 0, 24), [[32, 12], [0, 2]], ROT + 176 - 16, 0)
-    iota(R("gam", 24, 46), [[32, 11], [0, 2]], ROT + 176, 0)
-    iota(R("ones", 0, 512), [[0, 512]], 1, 0)
-    for b in range(4):
-        e = R("eb", 512 * b, 512 * b + 512)
-        emit("g", lambda: g.affine_select(ap(e), ap(R("ones", 0, 512)), [[-1, 512]], AO.is_equal, 0.0, b, 4), [R("ones", 0, 512)], [e])
-    ms(R("tbs", 224, 256), 0.0)
-    ms(R("tbs", 66, 96), 0.0)
-    for n, a in (("ttb", 0), ("ttb", 112), ("tf", 352), ("gl", 0), ("gl", 368), ("wa", 0), ("wa", 368), ("wb", 0), ("wb", 368),
-                 ("gb", 0), ("gb", 368), ("n1", 736), ("n2", 736), ("mf", 0), ("mo", 368)):
-        act(R(n, a, a + 16), R("tbs", 224, 240))
-    act(R("sm", 384, 400), R("tbs", 224, 240))
-    act(R("sm", 400, 432), R("tbs", 224, 256))
     def cf(i):
         return R("cf", i, i + 1)
 
@@ -212,72 +242,64 @@ def rank_program(g, core, T, topo):
     tr(R("lc", 0, 32), R("rc", 0, 32))
     copy(R("cf", 0, 3), R("ci", 1, 4))
     tt(ci(4), ci(1), ci(2), AO.add)
-    q_, par, i32, l32, odd = cf(0), cf(1), cf(2), R("lc", 0, 1), cf(3)
-    ts(cf(4), par, 97.0, AO.mult)
-    ts(cf(5), par, -127.0, AO.mult, 128.0, AO.add)
+    q_, par, i32, l22, ucol, odd = cf(0), cf(1), cf(2), R("lc", 0, 1), R("lc", 32, 33), cf(3)
+    ts(cf(4), par, 97.0, AO.mult, l22, AO.add)
+    ts(cf(5), par, -127.0, AO.mult, l22, AO.add)
     ts(ci(5), ci(4), 1, AO.bitwise_and)
-    tt(cf(6), cf(4), l32, AO.add)
-    tt(cf(7), cf(5), l32, AO.add)
+    tr(R("tc", 0, 160), R("tb", 0, 160))
+    ts(cf(6), cf(4), 224.0, AO.min)
+    ts(cf(7), cf(5), 128.0, AO.add, 224.0, AO.min)
     copy(odd, ci(5))
-    ts(cf(6), cf(6), 224.0, AO.min)
-    ts(cf(7), cf(7), 224.0, AO.min)
+    tr(R("lc", 32, 64), R("rc", 32, 64))
     ts(R("offi", 0, 22, 2), R("i2", 0, 22, 2), cf(6), AO.add)
     ts(R("offi", 1, 22, 2), R("i2", 1, 22, 2), cf(7), AO.add)
-    RM, THR, WT, NB = cf(8), cf(9), cf(19), cf(20)
+    ts(cf(10), odd, -23.0, AO.mult, 24.0, AO.add)
+    ts(cf(8), KEEP, -16.0, AO.mult, ucol, AO.add)
+    ts(R("upk", 0, 8, 2), R("i2", 24, 32, 2), ucol, AO.add)
+    tt(cf(11), cf(10), q_, AO.add)
+    ts(R("upk", 1, 8, 2), R("i2", 25, 32, 2), cf(8), AO.add)
+    ts(cf(12), cf(11), 16.0, AO.add, 45.0, AO.min)
+
+    P1, PP, PK, PK1, PO, PD, P2 = R("pk", 0, 2), R("pk", 2, 4), R("pk", 4, 6), R("pk", 4, 5), R("pk", 6, 7), R("pk", 8, 10), R("pk", 10, 12)
+    UN = R("cf", 11, 13)
 
     ts(R("tbs", 0, 66), R("tbi", 0, 66), float(-MID), AO.add)
     copy(R("opi", 0, 22), R("tbi", 0, 22))
     tr(R("ttb", 16, 112), R("tbs", 0, 96))
+    ts(PP, UN, 16.0, AO.mult, float(QP), AO.add)
     tr(R("tbs", 96, 224), R("ttb", 0, 128))
-    copy(R("tf", 0, 352), R("tbs", 0, 256), R("offi", 0, 22))
-    tr(R("wa", 16, 368), R("tf", 0, 352))
-    GAM = R("gam", 0, 46)
+    ts(PD, UN, 16.0, AO.mult, float(QD), AO.add)
+    both("tf", 16, R("tbs", 0, 256), "offi", 12)
+    qm(R("qu", 0, 128), R("su", 0, 128), R("ut", 0, 512))
+    tr(R("wa", 16, 368), R("tf", 16, 368))
+    UP = R("upk", 0, 8)
+    act(R("sd", 0, 128), R("su", 0, 128), UP)
+    emit("v", lambda: V.tensor_copy(T.qd[:, 0:128].bitcast(dt.uint32), T.qu[:, 0:128].bitcast(dt.uint32).indirect(ap(UP))),
+         [R("qu", 0, 128), UP], [R("qd", 0, 128)])
+    LK = R("wa", 16, 368)
+    GAB = R("gab", 0, 46)
 
-    def sm(i):
-        return R("sm", 48 * i, 48 * i + 46)
+    def turn(dst, srcb, a, b):
+        tr(R(dst, 384 + a, 384 + b), R(srcb, 16 + a, 16 + b))
+        e = 384 if b == C else b
+        tr(R(dst, a, e), R(srcb, a, e))
 
-    PM, PP, PK, PK1, PO, PD = R("pk", 0, 2), R("pk", 2, 4), R("pk", 4, 6), R("pk", 4, 5), R("pk", 6, 7), R("pk", 8, 10)
+    def pick(out, n, units, lst):
+        ts(R(out, 0, n), R(units, 0, 736), float(MID), AO.add, off=lst)
 
-    def prelinks(off):
-        act(R("gl", 16, 368), R("wa", 16, 368), off)
-
-    def prelinks2():
-        tr(R("glt", 0, 384), R("gl", 0, 384))
-        tr(R("glt", 384, 736), R("gl", 16, 368))
-
-    def prelinks3():
-        for o, pick, a in (("td", PD, 1088), ("tp", PP, 1440)):
-            ts(R(o, 0, 32), R("glt", 0, 736), float(MID), AO.add, off=pick)
-            act(R("wa", a, a + C), R("wa", 16, 368), R(o, 0, 22))
-
-    def prelinks4():
-        act(R("wr", 704, 1056), R("wa", 384, 736), R("td", 0, 22))
-        act(R("wr", 1056, 1408), R("wa", 384, 736), R("tp", 0, 22))
-
-    prelinks(R("opi", 0, 22))
-    act(R("wa", 736, 1088), R("wa", 16, 368))
-    ts(cf(10), odd, -23.0, AO.mult, 24.0, AO.add)
-    ts(THR, q_, 3.5, AO.is_ge, 1e28, AO.mult)
-    ts(cf(17), q_, 0.0, AO.is_equal, 352.0, AO.mult)
-    ts(cf(18), q_, 2.0, AO.is_equal, 1696.0, AO.mult)
-    tt(cf(11), cf(10), q_, AO.add)
-    ts(WT, cf(17), cf(18), AO.add, 352.0, AO.add)
-    ts(cf(12), cf(11), 16.0, AO.add, 45.0, AO.min)
-    ts(PP, R("cf", 11, 13), 16.0, AO.mult, 5.0, AO.add)
-    ts(PD, R("cf", 11, 13), 16.0, AO.mult, 6.0, AO.add)
-    copy(PM, R("cf", 11, 13))
     rest = [
-        lambda: ts(GAM, GAM, i32, AO.add),
-        lambda: ts(cf(21), q_, 2.0, AO.is_equal, -1024.0, AO.mult),
-        lambda: ts(cf(22), q_, 3.0, AO.is_equal, -176.0, AO.mult),
-        lambda: tt(NB, cf(21), cf(22), AO.add),
-        lambda: ts(RM, l32, 500.0, AO.is_lt),
-        lambda: ts(PK, R("cf", 11, 13), 16.0, AO.mult, 7.0, AO.add),
-        lambda: ts(cf(14), odd, 23.0, AO.mult, 12.0, AO.add),
+        lambda: copy(cf(13), q_),
+        lambda: ts(cf(14), q_, 16.0, AO.add, 21.0, AO.min),
+        lambda: ts(cf(15), par, 4.0, AO.mult, 3.0, AO.add),
+        lambda: ts(R("opm", 0, 22), R("tf", 16 + QP, 368, 16), float(MID), AO.add),
+        lambda: ts(P1, R("cf", 13, 15), 8.0, AO.mult, cf(15), AO.add),
+        lambda: ts(GAB, R("gam", 0, 46), i32, AO.add),
+        lambda: ts(P2, UN, 4.0, AO.mult, 3.0, AO.add),
+        lambda: ts(PK, UN, 16.0, AO.mult, float(QK), AO.add),
+        lambda: ts(cf(16), odd, 23.0, AO.mult, 12.0, AO.add),
         lambda: ms(cf(23), float(MID)),
-        lambda: tt(cf(15), cf(14), q_, AO.add),
-        lambda: ts(cf(16), cf(15), 45.0, AO.min, 16.0, AO.mult),
-        lambda: ts(PO, cf(16), 7.0, AO.add),
+        lambda: ts(cf(17), cf(16), q_, AO.add, 45.0, AO.min),
+        lambda: ts(PO, cf(17), 16.0, AO.mult, float(QK), AO.add),
     ]
 
     def fill(n):
@@ -285,44 +307,47 @@ def rank_program(g, core, T, topo):
             if rest:
                 rest.pop(0)()
 
+    def half(h):
+        return (0, F) if h == 0 else (F, C)
+
     def state_half(r, h):
-        lo, hi = (0, F) if h == 0 else (F, C)
+        lo, hi = half(h)
         qm(R("qx", lo, hi), R("sx", lo, hi), R("x%d" % r, 4 * lo, 4 * hi))
 
     def signs_mm(h):
-        lo, hi = (0, F) if h == 0 else (F, C)
-        mm(5 - h, F, R("qu", 0, 128), R("su", 0, 128), R("qx", lo, hi), R("sx", lo, hi))
+        lo, hi = half(h)
+        mm(5 - h, F, R("qd", 0, 128), R("sd", 0, 128), R("qx", lo, hi), R("sx", lo, hi))
 
     def signs_ts(h):
-        lo, hi = (0, F) if h == 0 else (F, C)
-        ts(R("bt", lo, hi), R("ps", 512 * (5 - h), 512 * (5 - h) + F), THR, AO.is_gt, WT, AO.mult)
+        lo, hi = half(h)
+        ts(R("bt", lo, hi), R("ps", 512 * (5 - h), 512 * (5 - h) + F), 0.0, AO.is_gt, WT, AO.mult)
 
-    def planes(r, h):
-        lo, hi = (0, F) if h == 0 else (F, C)
-        for t in range(4):
-            act(R("xp", C * t + lo, C * t + hi), R("x%d" % r, 4 * lo + t, 4 * hi, 4), scale=0.5)
+    def plane(r, h, t):
+        lo, hi = half(h)
+        act(R("xp", C * t + lo, C * t + hi), R("x%d" % r, 4 * lo + t, 4 * hi, 4), scale=0.5)
 
-    prelinks2()
-    prelinks3()
+    both("gl", 16, LK, "opi", 8)
     state_half(0, 1)
-    qm(R("qu", 0, 128), R("su", 0, 128), R("ut", 0, 512))
     state_half(0, 0)
-    tr(R("wa", 384, 736), R("tf", 1, 353))
+    act(R("wa", 736, 1088), LK)
     signs_mm(1)
     signs_mm(0)
+    turn("glt", "gl", 0, C)
+    fill(2)
+    pick("td", 32, "glt", PD)
+    pick("tp", 32, "glt", PP)
+    act(R("wa", 1088, 1440), LK, R("td", 0, 22))
+    fill(2)
     signs_ts(1)
     signs_ts(0)
+    act(R("wa", 1440, 1792), LK, R("tp", 0, 22))
+    tr(R("wa", 384, 736), R("tf", 14, 366))
+    fill(1)
 
     ALL = R("wa", 384, 1792)
     ALLB = R("wb", 16, 1088)
+    BT = R("bt", 0, C)
 
-    def turn(dst, srcb, a, b):
-        tr(R(dst, 384 + a, 384 + b), R(srcb, 16 + a, 16 + b))
-        e = 384 if b == C else b
-        tr(R(dst, a, e), R(srcb, a, e))
-
-    dst = T.cores[0]
-    offp = R("opi", 0, 22)
     for r in range(3):
         s = STEP[r]
         source, target = T.cores[(rank - s) % 8], T.cores[(rank + s) % 8]
@@ -335,68 +360,63 @@ def rank_program(g, core, T, topo):
         arrive(R("sin%d" % r, 0, F), "as%d" % r, n_all)
         X, XN = "x%d" % r, "x%d" % (r + 1)
 
-        k = 10
+        k = 22 if r == 0 else 10
         a = 16 * k
-        BT = R("bt", 0, C)
-        copy(R("gb", 16, 16 + a), BT, R(offp[0], 0, k))
-        act(R("gb", 16 + a, 368), BT, R(offp[0], k, 22))
-        turn("gt", "gb", 0, a)
-        turn("gt", "gb", a, C)
-        A0, A1 = R("gt", 0, 736, 16), R("gt", 1, 736, 16)
-        tt(sm(3), A0, A1, AO.add)
+        ts(R("gm", 0, a), BT, KEEP, AO.mult, START, AO.add, off=R("opm", 0, k))
+        if k < 22:
+            act(R("gm", a, C), BT, R("opm", k, 22), scale=KEEP, bias=START)
+            tr(R("g1", 0, a), R("gm", 0, a))
+            tr(R("g1", a, C), R("gm", a, C))
+        else:
+            tr(R("g1", 0, C), R("gm", 0, C))
         fill(1)
-        tt(sm(8), sm(3), GAM, AO.add)
+        scan(R("s1", 0, F), R("g1", 0, C, 2), R("so", 0, F))
         fill(1)
-        ts(R("o1", 0, 32), R("sm", 48 * 8, 48 * 9), float(-ROT - 176), AO.add, off=PM)
+        ts(R("o1", 0, 32), R("s1", 0, F), q_, AO.add, off=P1)
         fill(1)
         tt(R("wb", 16, 368), ALL, BT, AO.add, off=R("o1", 0, 22))
         if r == 0:
             act(R("wb", 736, 1088), R("wa", 736, 1088))
-            planes(0, 1)
+            for t in range(4):
+                plane(0, 1, t)
         else:
             act(R("wb", 384, 736), R("wr", 0, 1408), R("o1", 0, 22))
-        planes(r, 0)
         fill(1)
         turn("n1", "wb", 0, C)
         fill(1)
-        ts(R("op1", 0, 32), R("n1", 0, 736), float(MID), AO.add, off=PP)
+        pick("op1", 32, "n1", PP)
         fill(1)
 
-        k = 8 if r == 0 else 10
+        k = 8
         a = 16 * k
         CB = R("wb", 16, 368)
         act(R("gb", 16 + a, 368), CB, R("op1", k, 22), bias=NB)
         ts(R("gb", 16, 16 + a), CB, NB, AO.add, off=R("op1", 0, k))
-        turn("gt", "gb", 0, a)
         if r == 0:
-            tr(R("wb", 384, 736), R("n1", 385, 737))
+            tr(R("wb", 384, 736), R("n1", 382, 734))
+            for t in range(4):
+                plane(0, 0, t)
+        turn("gt", "gb", 0, a)
         turn("gt", "gb", a, C)
-        A2, A3, GP, GD = R("gt", 2, 736, 16), R("gt", 3, 736, 16), R("gt", 5, 736, 16), R("gt", 6, 736, 16)
-        tt(sm(1), GP, A3, AO.add)
-        tt(sm(2), GD, A3, AO.subtract)
-        tt(sm(3), GAM, A3, AO.add)
-        tt(sm(4), sm(1), sm(2), AO.max)
-        tt(sm(5), sm(3), A2, AO.subtract)
-        tt(sm(6), sm(4), A2, AO.add)
         fill(1)
-        tt(sm(8), sm(6), sm(5), AO.max)
+        copy(R("gt", 3, 736, 16), GAB)
         fill(1)
-        ts(R("o2", 0, 32), R("sm", 48 * 8, 48 * 9), -1024.0, AO.add, off=PM)
+        scan(R("s2", 0, 184), R("gt", 0, 736, 4), R("gt", 3, 736, 4))
         fill(1)
-        k = 10
+        ts(R("o2", 0, 32), R("s2", 0, 184), float(MID), AO.add, off=P2)
+        fill(1)
+        k = 8
         a = 16 * k
         act(R("wa", 16 + a, 368), ALLB, R("o2", k, 22), scale=RM)
         ts(R("wa", 16, 16 + a), ALLB, RM, AO.mult, off=R("o2", 0, k))
         turn("n2", "wa", 0, a)
         turn("n2", "wa", a, C)
-        fill(1)
+        fill(20)
         OP = "opn%d" % r
-        N2 = R("n2", 0, 736)
-        ts(R(OP, 0, 32), N2, float(MID), AO.add, off=PP)
+        pick(OP, 32, "n2", PP)
         KS = R("ks%d" % r, 0, 22)
-        copy(KS, R("n2", 384 + 7, 736, 16))
-        ts(R("ok", 0, 32), N2, float(MID), AO.add, off=PK)
-        offp = R(OP, 0, 22)
+        copy(KS, R("n2", 384 + QK, 736, 16))
+        pick("ok", 32, "n2", PK)
 
         for d, sr, ds, sem in ((source, R(OP, 0, 12), PIN, "ap%d" % r), (target, KS, R("kin%d" % r, 0, 22), "ak%d" % r)):
             ready("g", [sr])
@@ -405,9 +425,12 @@ def rank_program(g, core, T, topo):
             count["sent"] = count.get("sent", 0) + len(topo.engines(core, d))
 
         if not last:
-            tr(R("wa", 384, 736), R("n2", 385, 737))
-        fill(20)
-        for c, (k0, k1) in enumerate(((0, 12), (12, 22))):
+            ts(R("opm", 0, 22), R("n2", 384 + QP, 736, 16), float(MID), AO.add)
+            copy(R("n2", 384 + 1, 736, 16), R("n2", 384 + QP, 736, 16))
+            copy(R("n2", 384 + 3, 736, 16), KS)
+
+        RUNS = ((0, 14), (14, 22))
+        for c, (k0, k1) in enumerate(RUNS):
             lo, hi = 16 * k0, 16 * k1
             for t in range(4):
                 win = R("xp", C * t, C * t + C)
@@ -418,30 +441,40 @@ def rank_program(g, core, T, topo):
             for b in range(4):
                 mm(4 * c + b, hi - lo, R("wq", 128 * b, 128 * b + 128), R("wp", 128 * b, 128 * b + 128), R("qz", lo, hi), R("sz", lo, hi))
 
-        def evict(c, b):
-            lo, w = (0, 192) if c == 0 else (192, 160)
+        def evict(c, b, q):
+            lo, hi = 16 * RUNS[c][0], 16 * RUNS[c][1]
             bank = 512 * (4 * c + b)
-            act(R("hp", C * b + lo, C * b + lo + w), R("ps", bank, bank + w), scale=0.03125)
-
-        for b in range(3):
-            evict(0, b)
-        act(R("mf", 16, 208), R("wa", 16, 368), R("pin%d" % r, 0, 12))
-        evict(0, 3)
-        if r == 0:
-            for b in range(4):
-                qm(R("qe", 128 * b, 128 * b + 128), R("se", 128 * b, 128 * b + 128), R("eb", 512 * b, 512 * b + 512))
-        if r == 1:
-            qm(R("qv", 0, 128), R("sv", 0, 128), R("vt", 0, 512))
-        turn("gt", "mf", 0, 192)
-        ts(R("om", 0, 16), R("gt", 0, 736), float(MID), AO.add, off=PK1)
-        for b in range(4):
-            evict(1, b)
-            ft = R("ft", b, 4 * F, 4)
-            hw = R("hp", C * b, C * b + C)
-            if b < 3:
-                copy(ft, hw, R("om", 0, 11))
+            out, in_ = R("hp", C * b + lo, C * b + hi), R("ps", bank, bank + hi - lo)
+            if q == "s":
+                act(out, in_, scale=0.03125)
             else:
+                ts(out, in_, 0.03125, AO.mult)
+
+        def part(b, q):
+            ft, hw = R("ft", b, 4 * F, 4), R("hp", C * b, C * b + C)
+            if q == "s":
                 act(ft, hw, R("om", 0, 11))
+            else:
+                copy(ft, hw, R("om", 0, 11))
+
+        evict(0, 0, "s")
+        evict(0, 1, "s")
+        act(R("mf", 16, 208), LK, PIN)
+        evict(0, 2, "v")
+        evict(0, 3, "v")
+        evict(1, 0, "s")
+        turn("mt", "mf", 0, 192)
+        evict(1, 1, "s")
+        if r == 0:
+            ms(R("mt", 192, 384), 0.0)
+            ms(R("mt", 576, 736), 0.0)
+        pick("om", 16, "mt", PK1)
+        evict(1, 2, "s")
+        part(0, "v")
+        evict(1, 3, "s")
+        part(1, "v")
+        part(3, "s")
+        part(2, "v")
         qm(R("qf%d" % r, 0, F), R("sf%d" % r, 0, F), R("ft", 0, 4 * F))
 
         QF, SF = R("qf%d" % r, 0, F), R("sf%d" % r, 0, F)
@@ -452,40 +485,53 @@ def rank_program(g, core, T, topo):
         g.remote_dma(ap(R("sin%d" % r, 0, F)), ap(SF), T.sem["as%d" % r], T.sem["sent"], pid, rid, m)
         count["sent"] += 2 * n_all
 
+        copy(R("n1", 384 + QK, 736, 16), R("kin%d" % r, 0, 22))
         if not last:
-            prelinks(offp)
-        copy(R("n1", 384 + 7, 736, 16), R("kin%d" % r, 0, 22))
+            act(R("gl", 16, 368), LK, R(OP, 0, 22))
         tr(R("kr", 0, C), R("n1", 384, 736))
         act(R("mo", 176, 368), R("kr", 0, C), R(OP, 10, 22))
         if not last:
-            prelinks2()
-            prelinks3()
+            turn("glt", "gl", 0, C)
+            pick("td", 32, "glt", PD)
+            pick("tp", 32, "glt", PP)
+            act(R("wa", 1088, 1440), LK, R("td", 0, 22))
+            act(R("wa", 1440, 1792), LK, R("tp", 0, 22))
         tr(R("gt", 384 + 160, 736), R("mo", 176, 368))
         tr(R("gt", 192, 384), R("mo", 192, 384))
-        ts(R("oo", 0, 16), R("gt", 0, 736), float(MID), AO.add, off=PO)
+        if not last:
+            tr(R("wa", 384, 736), R("n2", 382, 734))
+        pick("oo", 16, "gt", PO)
+        if r == 0:
+            qm(R("qe", 0, 512), R("se", 0, 512), R("eb", 0, 2048))
         for t in range(4):
             tt(R(XN, 4 * F + t, 4 * C, 4), R("hp", C * t, C * t + C), R(X, 4 * F + t, 4 * C, 4), AO.add, off=R("oo", 0, 11))
         state_half(r + 1, 1)
         if not last:
-            planes(r + 1, 1)
-            prelinks4()
+            act(R("wr", 704, 1056), R("wa", 384, 736), R("td", 0, 22))
+            act(R("wr", 1056, 1408), R("wa", 384, 736), R("tp", 0, 22))
+            for t in range(4):
+                plane(r + 1, 1, t)
             signs_mm(1)
-            tr(R("wr", 0, 352), R("n2", 386, 738))
+            tr(R("wr", 0, 352), R("n2", 380, 732))
             if r == 0:
-                tr(R("wr", 352, 704), R("tf", 1, 353))
+                tr(R("wr", 352, 704), R("tf", 14, 366))
+            else:
+                qm(R("qv", 0, 128), R("sv", 0, 128), R("vt", 0, 512))
+            signs_ts(1)
         else:
             store(g, T, emit, ap, R, mm, act, ts, 1)
             lkt = R("lkt", 0, C)
-            act(lkt, R("wa", 16, 368), bias=cf(23))
-            for gr in range(8):
-                emit("y", lambda: g.sync.dma_start(T.lk[gr:gr + 1, :], T.lkt[16 * gr + 5:16 * gr + 8, :]), [lkt], [], "sty", 16)
+            act(lkt, LK, bias=cf(23))
+            for i, q in enumerate((QP, QD, QK)):
+                emit("y", lambda: g.sync.dma_start(T.lk[:, C * i:C * i + C], T.lkt[q:128:16, :]), [lkt], [], "sty", 16)
 
         for b in range(4):
             out = mm(b, F, R("qe", 128 * b, 128 * b + 128), R("se", 128 * b, 128 * b + 128), R("qin%d" % r, 0, F), R("sin%d" % r, 0, F))
             tt(R(XN, b, 4 * F, 4), out, R(X, b, 4 * F, 4), AO.add)
+            if not last:
+                plane(r + 1, 0, b)
         state_half(r + 1, 0)
         if not last:
-            signs_ts(1)
             signs_mm(0)
             signs_ts(0)
         else:

@@ -6,15 +6,15 @@ MID = 176
 ROT, DRAWN = 368, 720
 QP, QK, QD = 7, 9, 11
 LOW = -4096
+TINY = 2.0 ** -40
 B16, F32, I32, U16, U8, MXC = "bfloat16", "float32", "int32", "uint16", "uint8", "float8_e4m3fn_x4"
 
 SCRATCH = {
     "tbi": ("sbuf", [128, 96], I32), "tbs": ("sbuf", [128, 256], B16), "ttb": ("sbuf", [128, 128], B16), "tf": ("sbuf", [128, 384], B16),
-    "ones": ("sbuf", [128, 512], B16), "eb": ("sbuf", [128, 2048], B16), "qe": ("sbuf", [128, 512], MXC), "se": ("sbuf", [128, 512], U8),
-    "ci": ("sbuf", [128, 16], I32), "cf": ("sbuf", [128, 64], F32), "rc": ("sbuf", [128, 72], F32), "lc": ("sbuf", [128, 64], F32),
-    "tb": ("sbuf", [128, 160], F32), "tc": ("sbuf", [128, 160], F32),
-    "i2": ("sbuf", [128, 32], F32), "gam": ("sbuf", [128, 48], F32), "gab": ("sbuf", [128, 48], B16),
-    "offi": ("sbuf", [128, 24], U16), "pk": ("sbuf", [128, 16], U16), "upk": ("sbuf", [128, 8], U16),
+    "ones": ("sbuf", [128, 516], B16), "eb": ("sbuf", [128, 516], B16), "qe": ("sbuf", [128, 512], MXC), "se": ("sbuf", [128, 512], U8),
+    "cf": ("sbuf", [128, 16], F32), "tb": ("sbuf", [128, 488], F32), "tc": ("sbuf", [128, 480], F32),
+    "i2": ("sbuf", [128, 40], F32), "gam": ("sbuf", [128, 48], F32), "gab": ("sbuf", [128, 48], B16),
+    "offi": ("sbuf", [128, 24], U16), "pk": ("sbuf", [128, 24], U16), "upk": ("sbuf", [128, 8], U16),
     "wq": ("sbuf", [128, 512], MXC), "wp": ("sbuf", [128, 512], U8),
     "ut": ("sbuf", [128, 512], B16), "qu": ("sbuf", [128, 128], MXC), "su": ("sbuf", [128, 128], U8),
     "qd": ("sbuf", [128, 128], MXC), "sd": ("sbuf", [128, 128], U8),
@@ -23,19 +23,20 @@ SCRATCH = {
     "xp": ("sbuf", [128, 4 * C], B16), "hp": ("sbuf", [128, 4 * C], B16), "zp": ("sbuf", [128, 4 * C], B16), "zt": ("sbuf", [128, 4 * C], B16),
     "ft": ("sbuf", [128, 4 * F], B16),
     "qx": ("sbuf", [128, C], MXC), "sx": ("sbuf", [128, C], U8), "qz": ("sbuf", [128, C], MXC), "sz": ("sbuf", [128, C], U8),
-    "bt": ("sbuf", [128, C], B16), "wr": ("sbuf", [128, 1408], B16), "td": ("sbuf", [128, 32], U16), "tp": ("sbuf", [128, 32], U16),
-    "wa": ("sbuf", [128, 1792], B16), "wb": ("sbuf", [128, 1088], B16),
+    "bt": ("sbuf", [128, C], B16), "ww": ("sbuf", [128, 1776], B16), "wr": ("sbuf", [128, 1760], B16), "td": ("sbuf", [128, 64], U16),
+    "wa": ("sbuf", [128, 384], B16), "wb": ("sbuf", [128, 1088], B16),
     "gm": ("sbuf", [128, C], B16), "g1": ("sbuf", [128, C], B16), "so": ("sbuf", [128, F], B16), "s1": ("sbuf", [128, F], B16),
+    "sp": ("sbuf", [128, 384], B16), "s3": ("sbuf", [128, C], B16),
     "gb": ("sbuf", [128, 384], B16), "gl": ("sbuf", [128, 384], B16), "mf": ("sbuf", [128, 384], B16), "mo": ("sbuf", [128, 384], B16),
     "gt": ("sbuf", [128, 752], B16), "glt": ("sbuf", [128, 752], B16), "n1": ("sbuf", [128, 752], B16), "n2": ("sbuf", [128, 752], B16),
     "mt": ("sbuf", [128, 752], B16), "kr": ("sbuf", [128, C], B16), "s2": ("sbuf", [128, 184], F32),
-    "o1": ("sbuf", [128, 32], U16), "o2": ("sbuf", [128, 32], U16), "op1": ("sbuf", [128, 32], U16), "ok": ("sbuf", [128, 32], U16),
+    "o1": ("sbuf", [128, 32], U16), "o2": ("sbuf", [128, 32], U16), "op1": ("sbuf", [128, 32], U16),
     "opi": ("sbuf", [128, 32], U16), "opm": ("sbuf", [128, 32], U16), "om": ("sbuf", [128, 16], U16), "oo": ("sbuf", [128, 16], U16),
     "lkt": ("sbuf", [128, C], F32), "yt": ("sbuf", [128, C], F32),
     "ps": ("psum", [128, 4096], F32),
 }
 for _r in range(3):
-    SCRATCH["opn%d" % _r] = ("sbuf", [128, 32], U16)
+    SCRATCH["opn%d" % _r] = ("sbuf", [128, 64], U16)
     SCRATCH["ks%d" % _r] = ("sbuf", [128, 22], B16)
     SCRATCH["pin%d" % _r] = ("sbuf", [128, 22], U16)
     SCRATCH["kin%d" % _r] = ("sbuf", [128, 22], B16)
@@ -186,8 +187,15 @@ def rank_program(g, core, T, topo):
         eng = {"y": g.sync, "s": g.scalar}[q]
         emit(q, lambda: eng.dma_start(ap(out).bitcast(dt.uint8) if code else ap(out), in_ap), [], [out], sem, 16)
 
-    def iota(out, pattern, base, cm=0):
-        emit("g", lambda: g.iota(ap(out), pattern, base, cm, allow_small_or_imprecise_dtypes=True), [], [out])
+    def iota(out, pattern, base):
+        emit("g", lambda: g.iota(ap(out), pattern, base, 0, allow_small_or_imprecise_dtypes=True), [], [out])
+
+    def send(d, ds, sr, sem, code=False):
+        ready("g", [sr])
+        rid, pid = topo.addr(d, core)
+        a, b = (ap(ds).bitcast(dt.uint8), ap(sr).bitcast(dt.uint8)) if code else (ap(ds), ap(sr))
+        g.remote_dma(a, b, T.sem[sem], T.sem["sent"], pid, rid, topo.mask(core, d))
+        count["sent"] = count.get("sent", 0) + len(topo.engines(core, d))
 
     load("s", R("tbi", 0, 22), T.pl[:], "ldp")
     load("y", R("tbi", 22, 44), T.kl[:], "ldk")
@@ -195,73 +203,74 @@ def rank_program(g, core, T, topo):
     load("y", R("ut", 0, 512), T.u[:], "ldu")
     load("s", R("x0", 4 * F, 4 * C), T.x[:, 4 * F:4 * C], "ldx1")
     load("y", R("x0", 0, 4 * F), T.x[:, 0:4 * F], "ldx0")
-
-    ip = R("ci", 0, 1)
-    emit("g", lambda: g.iota(ap(ip), [[0, 1]], 0, 1), [], [ip])
-    iota(R("rc", 0, 32, 2), [[0, 16]], 1000)
-    iota(R("rc", 1, 19, 2), [[0, 3], [22, 3]], 0)
-    iota(R("rc", 17, 35, 2), [[0, 3], [22, 3]], 0)
-    iota(R("i2", 0, 22), [[2, 11], [0, 2]], 0)
-    iota(R("rc", 32, 64), [[0, 32]], 3)
-    iota(R("rc", 36, 64, 16), [[0, 2]], 2)
-    iota(R("rc", 34, 64, 8), [[0, 2], [16, 2]], 1)
-    iota(R("rc", 38, 64, 8), [[0, 2], [16, 2]], 0)
-    iota(R("i2", 24, 32), [[16, 8]], 0)
-    ms(R("tb", 0, 160), 0.0)
-    ms(R("tbs", 224, 256), 0.0)
-    ms(R("tbs", 66, 96), 0.0)
-    ms(R("so", 0, F), 2.0 * LOW)
-    iota(R("so", 0, F, 4), [[16, 22], [0, 2]], 0)
-    iota(R("gam", 0, 24), [[32, 12], [0, 2]], -16 - MID)
-    iota(R("gam", 24, 46), [[32, 11], [0, 2]], -MID)
-    iota(R("ones", 0, 512), [[0, 512]], 1)
-    for b in range(4):
-        e = R("eb", 512 * b, 512 * b + 512)
-        emit("g", lambda: g.affine_select(ap(e), ap(R("ones", 0, 512)), [[-1, 512]], AO.is_equal, 0.0, b, 4), [R("ones", 0, 512)], [e])
-    WT, KEEP, START, NB, RM = [R("tc", 32 * i, 32 * i + 1) for i in range(5)]
-    zero = R("tbs", 224, 240)
-    for i, q, st, c in ((0, 2, 8, 352), (0, 6, 8, 704), (0, 4, 16, LOW), (0, 8, 16, 704), (0, 12, 16, -352), (1, 2, 4, 1), (2, 0, 8, LOW), (4, 1, 2, 1)):
-        ms(R("tb", 32 * i + q, 32 * i + 32, st), float(c))
-    for q, c in ((0, LOW), (4, DRAWN), (8, -352), (15, LOW)):
-        act(R("tb", 96 + q, 128, 16), R("tbs", 224, 226), bias=float(c))
-    for n, a in (("ttb", 0), ("ttb", 112), ("tf", 0), ("gl", 0), ("gl", 368), ("wa", 0), ("wa", 368), ("wb", 0), ("wb", 368),
-                 ("gb", 0), ("gb", 368), ("mf", 0), ("mo", 368)):
-        act(R(n, a, a + 16), zero)
     load("y", R("wq", 0, 512), T.wc[:], "ldwc", True)
     load("y", R("wp", 0, 512), T.ws[:], "ldws")
     load("y", R("vt", 0, 512), T.v[:], "ldv")
 
-    def cf(i):
-        return R("cf", i, i + 1)
+    def tab(i, q=0, st=1, n=32):
+        return R("tb", 32 * i + q, 32 * i + n, st)
 
-    def ci(i):
-        return R("ci", i, i + 1)
-    ts(ci(1), ip, 15, AO.bitwise_and)
-    ts(ci(2), ip, 4, AO.arith_shift_right, 1, AO.bitwise_and)
-    ts(ci(3), ip, 31, AO.bitwise_and)
-    tr(R("lc", 0, 32), R("rc", 0, 32))
-    copy(R("cf", 0, 3), R("ci", 1, 4))
-    tt(ci(4), ci(1), ci(2), AO.add)
-    q_, par, i32, l22, ucol, odd = cf(0), cf(1), cf(2), R("lc", 0, 1), R("lc", 32, 33), cf(3)
-    ts(cf(4), par, 97.0, AO.mult, l22, AO.add)
-    ts(cf(5), par, -127.0, AO.mult, l22, AO.add)
-    ts(ci(5), ci(4), 1, AO.bitwise_and)
-    tr(R("tc", 0, 160), R("tb", 0, 160))
-    ts(cf(6), cf(4), 224.0, AO.min)
-    ts(cf(7), cf(5), 128.0, AO.add, 224.0, AO.min)
-    copy(odd, ci(5))
-    tr(R("lc", 32, 64), R("rc", 32, 64))
-    ts(R("offi", 0, 22, 2), R("i2", 0, 22, 2), cf(6), AO.add)
-    ts(R("offi", 1, 22, 2), R("i2", 1, 22, 2), cf(7), AO.add)
-    ts(cf(10), odd, -23.0, AO.mult, 24.0, AO.add)
-    ts(cf(8), KEEP, -16.0, AO.mult, ucol, AO.add)
-    ts(R("upk", 0, 8, 2), R("i2", 24, 32, 2), ucol, AO.add)
-    tt(cf(11), cf(10), q_, AO.add)
-    ts(R("upk", 1, 8, 2), R("i2", 25, 32, 2), cf(8), AO.add)
-    ts(cf(12), cf(11), 16.0, AO.add, 45.0, AO.min)
+    (EVEN, ODD, UCOL, PAIR, UNIT, WT, KEEP, START, NB, RM, Q16, P32, FIRST, UPPER, TWICE) = [R("tc", 32 * i, 32 * i + 1) for i in range(15)]
+    zero = R("tbs", 224, 240)
+    ms(R("tbs", 224, 256), 0.0)
+    ms(R("tbs", 66, 96), 0.0)
+    ms(tab(0, 0, 2, 64), 224.0)
+    for i, base in enumerate((0, 97, 128, 1)):
+        iota(R("tb", 16 * i + 1, 16 * i + 19, 2), [[0, 3], [22, 3]], base)
+    iota(R("i2", 0, 22), [[2, 11], [0, 2]], 0)
+    iota(tab(2), [[0, 2], [16, 2], [0, 8]], 1)
+    iota(R("i2", 24, 32), [[16, 8]], 0)
+    ms(tab(3), -16.0)
+    ms(tab(5, 0, 1, 160), 0.0)
+    ms(tab(3, 0, 4), 0.0)
+    for i, a, b, c, d in ((4, [[2, 8], [-22, 2]], 24, [[2, 8], [24, 2]], 1), (13, [[2, 8], [24, 2]], 12, [[2, 8], [-22, 2]], 35),
+                          (14, [[2, 4], [-22, 2], [0, 2]], 24, [[2, 4], [24, 2], [0, 2]], 1)):
+        iota(tab(i, 0, 1, 16), a, b)
+        iota(tab(i, 16), c, d)
+    iota(tab(10), [[0, 2], [1, 16]], 0)
+    iota(tab(11), [[1, 32]], 0)
+    iota(tab(12), [[4, 2], [8, 16]], 3)
+    for i, q, st, c in ((5, 1, 8, -704 * TINY), (5, 2, 8, -1056), (5, 3, 8, 704 * TINY), (5, 5, 8, 352 * TINY), (5, 6, 8, -352),
+                        (5, 4, 16, LOW), (5, 8, 16, 704), (5, 12, 16, -352), (6, 2, 4, 1), (6, 1, 2, 1 / TINY), (9, 1, 2, 1)):
+        ms(tab(i, q, st), float(c))
 
-    P1, PP, PK, PK1, PO, PD, P2 = R("pk", 0, 2), R("pk", 2, 4), R("pk", 4, 6), R("pk", 4, 5), R("pk", 6, 7), R("pk", 8, 10), R("pk", 10, 12)
-    UN = R("cf", 11, 13)
+    def pads(*where):
+        for n, a in where:
+            act(R(n, a, a + 16), zero)
+    pads(("ttb", 0), ("ttb", 112))
+    for i, q, st, c in ((7, 0, 8, LOW), (7, 1, 8, 352), (7, 2, 8, 352), (7, 3, 8, -352), (7, 5, 8, -352),
+                        (8, 0, 16, LOW), (8, 4, 16, DRAWN), (8, 8, 16, -352), (8, 15, 16, LOW)):
+        act(tab(i, q, st), R("tbs", 224, 224 + 32 // st), bias=float(c))
+    pads(("tf", 0), ("gl", 0), ("gl", 368), ("wa", 0), ("wa", 368), ("wb", 0), ("wb", 368), ("gb", 0), ("gb", 368))
+    tr(R("tc", 0, 64), tab(0, 0, 1, 64))
+    for q, st, c in ((2, 16, 0), (5, 16, 0), (10, 16, 16), (13, 16, 16), (4, 4, 3), (4, 16, 2)):
+        ms(tab(2, q, st), float(c))
+    ts(R("offi", 0, 22, 2), R("i2", 0, 22, 2), EVEN, AO.add)
+    ts(R("offi", 1, 22, 2), R("i2", 1, 22, 2), ODD, AO.add)
+    tr(R("tc", 64, 160), tab(2, 0, 1, 96))
+    tr(R("tc", 160, 320), tab(5, 0, 1, 160))
+
+    def run(i):
+        a = C * (0, 1, 3, 4)[i // 2]
+        return R("wr", a, a + C) if i % 2 else R("ww", 16 + a, 16 + a + C)
+
+    iota(R("so", 0, F), [[0, F]], 2 * LOW)
+    iota(R("ww", 16 + 2 * C, 16 + 3 * C), [[0, C]], 0)
+    iota(R("so", 0, F, 4), [[16, 22], [0, 2]], 0)
+    iota(R("gam", 0, 24), [[32, 12], [0, 2]], -16 - MID)
+    iota(R("gam", 24, 46), [[32, 11], [0, 2]], -MID)
+    iota(R("sp", 0, 384), [[0, 384]], 2 * LOW)
+    iota(R("wr", 2 * C, 3 * C), [[0, C]], 0)
+    one, e = R("ones", 0, 516), R("eb", 0, 516)
+    iota(one, [[0, 516]], 1)
+    emit("g", lambda: g.affine_select(ap(e), ap(one), [[-1, 516]], AO.is_equal, 0.0, 3, 4), [one], [e])
+
+    P1, PD, PP, PK, PK1, PO, P2 = R("pk", 0, 2), R("pk", 2, 4), R("pk", 4, 6), R("pk", 6, 8), R("pk", 6, 7), R("pk", 8, 9), R("pk", 10, 12)
+    P3, PP3, PD3 = R("pk", 22, 24), R("pk", 14, 17), R("pk", 18, 21)
+    UN, UN3, UP = R("cf", 0, 2), R("cf", 2, 5), R("upk", 0, 8)
+    ts(UN, R("i2", 24, 26), UNIT, AO.add, 45.0, AO.min)
+    ts(R("upk", 0, 8, 2), R("i2", 24, 32, 2), UCOL, AO.add)
+    ts(R("upk", 1, 8, 2), R("i2", 25, 32, 2), PAIR, AO.add, UCOL, AO.add)
 
     ts(R("tbs", 0, 66), R("tbi", 0, 66), float(-MID), AO.add)
     copy(R("opi", 0, 22), R("tbi", 0, 22))
@@ -269,37 +278,43 @@ def rank_program(g, core, T, topo):
     ts(PP, UN, 16.0, AO.mult, float(QP), AO.add)
     tr(R("tbs", 96, 224), R("ttb", 0, 128))
     ts(PD, UN, 16.0, AO.mult, float(QD), AO.add)
-    both("tf", 16, R("tbs", 0, 256), "offi", 12)
+    both("tf", 16, R("tbs", 0, 256), "offi", 10)
     qm(R("qu", 0, 128), R("su", 0, 128), R("ut", 0, 512))
     tr(R("wa", 16, 368), R("tf", 16, 368))
-    UP = R("upk", 0, 8)
     act(R("sd", 0, 128), R("su", 0, 128), UP)
     emit("v", lambda: V.tensor_copy(T.qd[:, 0:128].bitcast(dt.uint32), T.qu[:, 0:128].bitcast(dt.uint32).indirect(ap(UP))),
          [R("qu", 0, 128), UP], [R("qd", 0, 128)])
     LK = R("wa", 16, 368)
     GAB = R("gab", 0, 46)
 
-    def turn(dst, srcb, a, b):
-        tr(R(dst, 384 + a, 384 + b), R(srcb, 16 + a, 16 + b))
+    def turn(dst, srcb, a, b, at=0):
+        tr(R(dst, 384 + a, 384 + b), R(srcb, at + 16 + a, at + 16 + b))
         e = 384 if b == C else b
-        tr(R(dst, a, e), R(srcb, a, e))
+        tr(R(dst, a, e), R(srcb, at + a, at + e))
 
     def pick(out, n, units, lst):
         ts(R(out, 0, n), R(units, 0, 736), float(MID), AO.add, off=lst)
 
+    def unpacker(b):
+        qm(R("qe", 128 * b, 128 * b + 128), R("se", 128 * b, 128 * b + 128), R("eb", 3 - b, 515 - b))
+
     rest = [
-        lambda: copy(cf(13), q_),
-        lambda: ts(cf(14), q_, 16.0, AO.add, 21.0, AO.min),
-        lambda: ts(cf(15), par, 4.0, AO.mult, 3.0, AO.add),
         lambda: ts(R("opm", 0, 22), R("tf", 16 + QP, 368, 16), float(MID), AO.add),
-        lambda: ts(P1, R("cf", 13, 15), 8.0, AO.mult, cf(15), AO.add),
-        lambda: ts(GAB, R("gam", 0, 46), i32, AO.add),
+        lambda: ts(R("cf", 6, 8), R("i2", 24, 26), 8.0, AO.mult, FIRST, AO.add),
+        lambda: ms(R("cf", 9, 10), float(MID)),
+        lambda: ts(P1, R("cf", 6, 8), 175.0, AO.min),
+        lambda: ts(GAB, R("gam", 0, 46), P32, AO.add),
         lambda: ts(P2, UN, 4.0, AO.mult, 3.0, AO.add),
         lambda: ts(PK, UN, 16.0, AO.mult, float(QK), AO.add),
-        lambda: ts(cf(16), odd, 23.0, AO.mult, 12.0, AO.add),
-        lambda: ms(cf(23), float(MID)),
-        lambda: ts(cf(17), cf(16), q_, AO.add, 45.0, AO.min),
-        lambda: ts(PO, cf(17), 16.0, AO.mult, float(QK), AO.add),
+        lambda: ts(R("cf", 8, 9), UPPER, 45.0, AO.min),
+        lambda: ts(R("cf", 10, 13), R("i2", 24, 27), 0.5, AO.mult, TWICE, AO.add),
+        lambda: ts(PO, R("cf", 8, 9), 16.0, AO.mult, float(QK), AO.add),
+        lambda: ts(UN3, R("cf", 10, 13), 45.0, AO.min, 16.0, AO.mult),
+        lambda: ts(P3, P1, 2.0, AO.mult),
+        lambda: ts(PP3, UN3, float(QP), AO.add),
+        lambda: ts(PD3, UN3, float(QD), AO.add),
+        lambda: copy(R("sp", 1, C, 16), R("tbs", 0, 22)),
+        lambda: copy(R("sp", 9, C, 16), R("tbs", 0, 22)),
     ]
 
     def fill(n):
@@ -328,23 +343,23 @@ def rank_program(g, core, T, topo):
 
     both("gl", 16, LK, "opi", 8)
     state_half(0, 1)
+    act(run(4), LK)
+    act(R("wb", 736, 1088), LK)
+    turn("glt", "gl", 0, C)
+    fill(1)
+    pick("td", 64, "glt", R("pk", 2, 6))
     state_half(0, 0)
-    act(R("wa", 736, 1088), LK)
     signs_mm(1)
     signs_mm(0)
-    turn("glt", "gl", 0, C)
-    fill(2)
-    pick("td", 32, "glt", PD)
-    pick("tp", 32, "glt", PP)
-    act(R("wa", 1088, 1440), LK, R("td", 0, 22))
-    fill(2)
+    act(run(2), LK, R("td", 0, 22))
+    tr(R("tc", 320, 480), tab(10, 0, 1, 160))
     signs_ts(1)
-    signs_ts(0)
-    act(R("wa", 1440, 1792), LK, R("tp", 0, 22))
-    tr(R("wa", 384, 736), R("tf", 14, 366))
+    act(run(0), LK, R("td", 32, 54))
     fill(1)
+    signs_ts(0)
+    fill(2)
 
-    ALL = R("wa", 384, 1792)
+    ALL, TURNED = R("ww", 16, 16 + 5 * C), R("wr", 0, 5 * C)
     ALLB = R("wb", 16, 1088)
     BT = R("bt", 0, C)
 
@@ -360,32 +375,37 @@ def rank_program(g, core, T, topo):
         arrive(R("sin%d" % r, 0, F), "as%d" % r, n_all)
         X, XN = "x%d" % r, "x%d" % (r + 1)
 
-        k = 22 if r == 0 else 10
+        k = 14 if r == 0 else 10
         a = 16 * k
         ts(R("gm", 0, a), BT, KEEP, AO.mult, START, AO.add, off=R("opm", 0, k))
-        if k < 22:
-            act(R("gm", a, C), BT, R("opm", k, 22), scale=KEEP, bias=START)
-            tr(R("g1", 0, a), R("gm", 0, a))
-            tr(R("g1", a, C), R("gm", a, C))
-        else:
-            tr(R("g1", 0, C), R("gm", 0, C))
+        act(R("gm", a, C), BT, R("opm", k, 22), scale=KEEP, bias=START)
+        if r == 0:
+            tr(run(6), R("tf", 14, 366))
+        for t in range(3 if r else 0):
+            plane(r, 1, t)
+        tr(R("g1", 0, a), R("gm", 0, a))
+        tr(R("g1", a, C), R("gm", a, C))
         fill(1)
         scan(R("s1", 0, F), R("g1", 0, C, 2), R("so", 0, F))
+        if r:
+            scan(R("s3", 0, C), R("g1", 0, C), R("sp", 0, C))
         fill(1)
-        ts(R("o1", 0, 32), R("s1", 0, F), q_, AO.add, off=P1)
+        ts(R("o1", 0, 32), R("s1", 0, F), Q16, AO.add, 3.0 * C, AO.add, off=P1)
+        if r:
+            ts(R("op1", 0, 32), R("s3", 0, C), float(MID), AO.add, off=P3)
         fill(1)
         tt(R("wb", 16, 368), ALL, BT, AO.add, off=R("o1", 0, 22))
         if r == 0:
-            act(R("wb", 736, 1088), R("wa", 736, 1088))
+            pads(("mf", 0), ("mo", 368), ("ww", 0))
             for t in range(4):
                 plane(0, 1, t)
+            fill(1)
+            turn("n1", "wb", 0, C)
+            fill(1)
+            pick("op1", 32, "n1", PP)
+            fill(1)
         else:
-            act(R("wb", 384, 736), R("wr", 0, 1408), R("o1", 0, 22))
-        fill(1)
-        turn("n1", "wb", 0, C)
-        fill(1)
-        pick("op1", 32, "n1", PP)
-        fill(1)
+            act(R("wb", 384, 736), TURNED, R("o1", 0, 22))
 
         k = 8
         a = 16 * k
@@ -396,6 +416,8 @@ def rank_program(g, core, T, topo):
             tr(R("wb", 384, 736), R("n1", 382, 734))
             for t in range(4):
                 plane(0, 0, t)
+        else:
+            plane(r, 1, 3)
         turn("gt", "gb", 0, a)
         turn("gt", "gb", a, C)
         fill(1)
@@ -405,38 +427,30 @@ def rank_program(g, core, T, topo):
         fill(1)
         ts(R("o2", 0, 32), R("s2", 0, 184), float(MID), AO.add, off=P2)
         fill(1)
-        k = 8
-        a = 16 * k
         act(R("wa", 16 + a, 368), ALLB, R("o2", k, 22), scale=RM)
         ts(R("wa", 16, 16 + a), ALLB, RM, AO.mult, off=R("o2", 0, k))
+        fill(1)
         turn("n2", "wa", 0, a)
         turn("n2", "wa", a, C)
-        fill(20)
+        fill(1)
         OP = "opn%d" % r
-        pick(OP, 32, "n2", PP)
+        pick(OP, 64, "n2", R("pk", 4, 8))
         KS = R("ks%d" % r, 0, 22)
-        copy(KS, R("n2", 384 + QK, 736, 16))
-        pick("ok", 32, "n2", PK)
-
-        for d, sr, ds, sem in ((source, R(OP, 0, 12), PIN, "ap%d" % r), (target, KS, R("kin%d" % r, 0, 22), "ak%d" % r)):
-            ready("g", [sr])
-            rid, pid = topo.addr(d, core)
-            g.remote_dma(ap(ds), ap(sr), T.sem[sem], T.sem["sent"], pid, rid, topo.mask(core, d))
-            count["sent"] = count.get("sent", 0) + len(topo.engines(core, d))
-
-        if not last:
-            ts(R("opm", 0, 22), R("n2", 384 + QP, 736, 16), float(MID), AO.add)
-            copy(R("n2", 384 + 1, 736, 16), R("n2", 384 + QP, 736, 16))
-            copy(R("n2", 384 + 3, 736, 16), KS)
+        send(source, PIN, R(OP, 0, 12), "ap%d" % r)
 
         RUNS = ((0, 14), (14, 22))
         for c, (k0, k1) in enumerate(RUNS):
             lo, hi = 16 * k0, 16 * k1
-            for t in range(4):
+            for t, j0, j1 in ([(3, 0, 6), (0, 0, 14), (1, 0, 14), (2, 0, 14), (3, 6, 14)] if c == 0 else [(t, k0, k1) for t in range(4)]):
                 win = R("xp", C * t, C * t + C)
-                zp = R("zp", C * t + lo, C * t + hi)
-                act(zp, win, R(OP, k0, k1))
-                tt(R("zt", 4 * lo + t, 4 * hi, 4), win, zp, AO.add, off=R("ok", k0, k1))
+                zp = R("zp", C * t + 16 * j0, C * t + 16 * j1)
+                (copy if j1 == 6 else act)(zp, win, R(OP, j0, j1))
+                tt(R("zt", 64 * j0 + t, 64 * j1, 4), win, zp, AO.add, off=R(OP, 32 + j0, 32 + j1))
+            if c == 0:
+                copy(KS, R("n2", 384 + QK, 736, 16))
+                send(target, R("kin%d" % r, 0, 22), KS, "ak%d" % r)
+            elif not last:
+                ts(R("opm", 0, 22), R("n2", 384 + QP, 736, 16), float(MID), AO.add)
             qm(R("qz", lo, hi), R("sz", lo, hi), R("zt", 4 * lo, 4 * hi))
             for b in range(4):
                 mm(4 * c + b, hi - lo, R("wq", 128 * b, 128 * b + 128), R("wp", 128 * b, 128 * b + 128), R("qz", lo, hi), R("sz", lo, hi))
@@ -450,78 +464,86 @@ def rank_program(g, core, T, topo):
             else:
                 ts(out, in_, 0.03125, AO.mult)
 
-        def part(b, q):
-            ft, hw = R("ft", b, 4 * F, 4), R("hp", C * b, C * b + C)
+        def part(b, q, j0=0, j1=11):
+            ft, hw = R("ft", 64 * j0 + b, 64 * j1, 4), R("hp", C * b, C * b + C)
             if q == "s":
-                act(ft, hw, R("om", 0, 11))
+                act(ft, hw, R("om", j0, j1))
             else:
-                copy(ft, hw, R("om", 0, 11))
+                copy(ft, hw, R("om", j0, j1))
 
+        if r:
+            act(R("mf", 16, 208), LK, PIN)
         evict(0, 0, "s")
         evict(0, 1, "s")
-        act(R("mf", 16, 208), LK, PIN)
-        evict(0, 2, "v")
+        if r:
+            turn("glt", "mf", 0, 192)
+        else:
+            act(R("mf", 16, 208), LK, PIN)
+            unpacker(0)
+        evict(0, 2, "s")
         evict(0, 3, "v")
-        evict(1, 0, "s")
-        turn("mt", "mf", 0, 192)
-        evict(1, 1, "s")
         if r == 0:
-            ms(R("mt", 192, 384), 0.0)
-            ms(R("mt", 576, 736), 0.0)
-        pick("om", 16, "mt", PK1)
-        evict(1, 2, "s")
-        part(0, "v")
-        evict(1, 3, "s")
-        part(1, "v")
-        part(3, "s")
+            turn("glt", "mf", 0, 192)
+            evict(1, 0, "v")
+        pick("om", 16, "glt", PK1)
+        if r:
+            evict(1, 0, "v")
+        evict(1, 1, "v")
+        part(0, "s")
+        evict(1, 2, "v")
+        evict(1, 3, "v")
+        part(1, "s")
         part(2, "v")
-        qm(R("qf%d" % r, 0, F), R("sf%d" % r, 0, F), R("ft", 0, 4 * F))
-
+        part(3, "v", 0, 6)
+        part(3, "s", 6, 11)
         QF, SF = R("qf%d" % r, 0, F), R("sf%d" % r, 0, F)
-        ready("g", [QF, SF])
-        rid, pid = topo.addr(target, core)
-        m = topo.mask(core, target)
-        g.remote_dma(ap(R("qin%d" % r, 0, F)).bitcast(dt.uint8), ap(QF).bitcast(dt.uint8), T.sem["ac%d" % r], T.sem["sent"], pid, rid, m)
-        g.remote_dma(ap(R("sin%d" % r, 0, F)), ap(SF), T.sem["as%d" % r], T.sem["sent"], pid, rid, m)
-        count["sent"] += 2 * n_all
+        qm(QF, SF, R("ft", 0, 4 * F))
 
-        copy(R("n1", 384 + QK, 736, 16), R("kin%d" % r, 0, 22))
+        send(target, R("qin%d" % r, 0, F), QF, "ac%d" % r, True)
+        send(target, R("sin%d" % r, 0, F), SF, "as%d" % r)
+
+        act(R("n1", 384 + QK, 736, 16), R("kin%d" % r, 0, 22))
         if not last:
             act(R("gl", 16, 368), LK, R(OP, 0, 22))
         tr(R("kr", 0, C), R("n1", 384, 736))
         act(R("mo", 176, 368), R("kr", 0, C), R(OP, 10, 22))
         if not last:
+            act(R("n2", 384 + 1, 736, 16), R("n2", 384 + QP, 736, 16))
+            act(R("n2", 384 + 3, 736, 16), R("n2", 384 + QK, 736, 16))
             turn("glt", "gl", 0, C)
-            pick("td", 32, "glt", PD)
-            pick("tp", 32, "glt", PP)
-            act(R("wa", 1088, 1440), LK, R("td", 0, 22))
-            act(R("wa", 1440, 1792), LK, R("tp", 0, 22))
+            pick("td", 64, "glt", R("pk", 2, 6))
+        else:
+            qm(R("qv", 0, 128), R("sv", 0, 128), R("vt", 0, 512))
         tr(R("gt", 384 + 160, 736), R("mo", 176, 368))
         tr(R("gt", 192, 384), R("mo", 192, 384))
         if not last:
-            tr(R("wa", 384, 736), R("n2", 382, 734))
+            tr(run(6), R("n2", 382, 734))
+            act(run(2), LK, R("td", 0, 22))
+            act(run(0), LK, R("td", 32, 54))
+            act(run(3), run(6), R("td", 0, 22))
+            act(run(1), run(6), R("td", 32, 54))
+            act(R("sp", 0, 384, 8), R("n2", 0, 736), PD3)
+        if r == 0:
+            unpacker(1)
         pick("oo", 16, "gt", PO)
         if r == 0:
-            qm(R("qe", 0, 512), R("se", 0, 512), R("eb", 0, 2048))
+            unpacker(2)
         for t in range(4):
             tt(R(XN, 4 * F + t, 4 * C, 4), R("hp", C * t, C * t + C), R(X, 4 * F + t, 4 * C, 4), AO.add, off=R("oo", 0, 11))
+        if r == 0:
+            unpacker(3)
         state_half(r + 1, 1)
         if not last:
-            act(R("wr", 704, 1056), R("wa", 384, 736), R("td", 0, 22))
-            act(R("wr", 1056, 1408), R("wa", 384, 736), R("tp", 0, 22))
-            for t in range(4):
-                plane(r + 1, 1, t)
-            signs_mm(1)
-            tr(R("wr", 0, 352), R("n2", 380, 732))
+            turn("mt", "ww", 0, C, C)
+            turn("glt", "ww", 0, C)
             if r == 0:
-                tr(R("wr", 352, 704), R("tf", 14, 366))
-            else:
-                qm(R("qv", 0, 128), R("sv", 0, 128), R("vt", 0, 512))
-            signs_ts(1)
+                tr(run(5), R("tf", 14, 366))
+            act(R("sp", 3, 384, 8), R("mt", 0, 736), PP3)
+            act(R("sp", 2, 384, 8), R("glt", 0, 736), PP3)
         else:
             store(g, T, emit, ap, R, mm, act, ts, 1)
             lkt = R("lkt", 0, C)
-            act(lkt, LK, bias=cf(23))
+            act(lkt, LK, bias=R("cf", 9, 10))
             for i, q in enumerate((QP, QD, QK)):
                 emit("y", lambda: g.sync.dma_start(T.lk[:, C * i:C * i + C], T.lkt[q:128:16, :]), [lkt], [], "sty", 16)
 
@@ -530,9 +552,13 @@ def rank_program(g, core, T, topo):
             tt(R(XN, b, 4 * F, 4), out, R(X, b, 4 * F, 4), AO.add)
             if not last:
                 plane(r + 1, 0, b)
+        if not last:
+            signs_mm(1)
         state_half(r + 1, 0)
         if not last:
             signs_mm(0)
+            signs_ts(1)
+            tr(run(7), R("n2", 380, 732))
             signs_ts(0)
         else:
             store(g, T, emit, ap, R, mm, act, ts, 0)

@@ -10,7 +10,7 @@ TINY = 2.0 ** -40
 B16, F32, I32, U16, U8, MXC = "bfloat16", "float32", "int32", "uint16", "uint8", "float8_e4m3fn_x4"
 
 SCRATCH = {
-    "tbi": ("sbuf", [128, 96], I32), "tbs": ("sbuf", [128, 256], B16), "ttb": ("sbuf", [128, 128], B16), "tf": ("sbuf", [128, 384], B16),
+    "tbi": ("sbuf", [128, 24], I32), "raw": ("sbuf", [128, C], I32), "tbs": ("sbuf", [128, 16], B16), "tf": ("sbuf", [128, 384], B16),
     "ones": ("sbuf", [128, 516], B16), "eb": ("sbuf", [128, 516], B16), "qe": ("sbuf", [128, 512], MXC), "se": ("sbuf", [128, 512], U8),
     "cf": ("sbuf", [128, 16], F32), "tb": ("sbuf", [128, 488], F32), "tc": ("sbuf", [128, 480], F32),
     "i2": ("sbuf", [128, 40], F32), "gam": ("sbuf", [128, 48], F32), "gab": ("sbuf", [128, 48], B16),
@@ -45,7 +45,7 @@ for _r in range(3):
     SCRATCH["qin%d" % _r] = ("sbuf", [128, F], MXC)
     SCRATCH["sin%d" % _r] = ("sbuf", [128, F], U8)
 SEMAPHORES = ["cv", "cs", "ct", "cg", "sent", "sty", "sta",
-              "ldp", "ldd", "ldk", "ldx0", "ldx1", "ldu", "ldv", "ldwc", "ldws"]
+              "ldp", "lda", "ldb", "ldx", "ldu", "ldv", "ldwc", "ldws"]
 SEMAPHORES += [k + str(r) for r in range(3) for k in ("ap", "ak", "ac", "as")]
 
 
@@ -70,7 +70,9 @@ def make_tracker(g, T):
     def note(r, write, tok):
         r = span(r)
         h = hist.setdefault(r[0], [])
-        if write and r[3] == 1:
+        if r[3] == 0:
+            r = r[:3] + (1,)
+        elif write and r[3] == 1:
             h[:] = [e for e in h if not (r[1] <= e[0][1] and e[0][2] <= r[2])]
         h.append((r, write, tok))
 
@@ -197,12 +199,18 @@ def rank_program(g, core, T, topo):
         g.remote_dma(a, b, T.sem[sem], T.sem["sent"], pid, rid, topo.mask(core, d))
         count["sent"] = count.get("sent", 0) + len(topo.engines(core, d))
 
+    RAW = R("raw", 0, C)
+    emit("v", lambda: V.memset(ap(RAW), MID), [], [RAW])
     load("s", R("tbi", 0, 22), T.pl[:], "ldp")
-    load("y", R("tbi", 22, 44), T.kl[:], "ldk")
-    load("s", R("tbi", 44, 66), T.dl[:], "ldd")
-    load("y", R("ut", 0, 512), T.u[:], "ldu")
-    load("s", R("x0", 4 * F, 4 * C), T.x[:, 4 * F:4 * C], "ldx1")
-    load("y", R("x0", 0, 4 * F), T.x[:, 0:4 * F], "ldx0")
+    for q, eng, sem, rows in (("s", S, "lda", ((QP, T.pl), (QD, T.dl))), ("y", g.sync, "ldb", ((QK, T.kl), (QD - 6, T.dl), (QK - 6, T.kl)))):
+        ready(q, [RAW])
+        for c, t in rows:
+            eng.dma_start(T.raw[c:128:16, :], t[:]).then_inc(T.sem[sem], 16)
+    arrive(RAW, "lda", 32)
+    arrive(R("raw", 0, C, 0), "ldb", 48)
+    load("s", R("ut", 0, 512), T.u[:], "ldu")
+    load("y", R("x0", 0, 4 * C), T.x[:], "ldx")
+    ready("y", [R("x0", 0, 4 * C)])
     load("y", R("wq", 0, 512), T.wc[:], "ldwc", True)
     load("y", R("wp", 0, 512), T.ws[:], "ldws")
     load("y", R("vt", 0, 512), T.v[:], "ldv")
@@ -210,14 +218,11 @@ def rank_program(g, core, T, topo):
     def tab(i, q=0, st=1, n=32):
         return R("tb", 32 * i + q, 32 * i + n, st)
 
-    (EVEN, ODD, UCOL, PAIR, UNIT, WT, KEEP, START, NB, RM, Q16, P32, FIRST, UPPER, TWICE) = [R("tc", 32 * i, 32 * i + 1) for i in range(15)]
-    zero = R("tbs", 224, 240)
-    ms(R("tbs", 224, 256), 0.0)
-    ms(R("tbs", 66, 96), 0.0)
-    ms(tab(0, 0, 2, 64), 224.0)
-    for i, base in enumerate((0, 97, 128, 1)):
-        iota(R("tb", 16 * i + 1, 16 * i + 19, 2), [[0, 3], [22, 3]], base)
-    iota(R("i2", 0, 22), [[2, 11], [0, 2]], 0)
+    (ROW, UCOL, PAIR, UNIT, WT, KEEP, START, NB, RM, Q16, P32, FIRST, UPPER, TWICE) = [R("tc", 32 * i, 32 * i + 1) for i in range(1, 15)]
+    zero = R("tbs", 0, 16)
+    ms(zero, 0.0)
+    iota(tab(1), [[0, 2], [22, 16]], 0)
+    iota(R("i2", 0, 22), [[1, 22]], 0)
     iota(tab(2), [[0, 2], [16, 2], [0, 8]], 1)
     iota(R("i2", 24, 32), [[16, 8]], 0)
     ms(tab(3), -16.0)
@@ -237,16 +242,14 @@ def rank_program(g, core, T, topo):
     def pads(*where):
         for n, a in where:
             act(R(n, a, a + 16), zero)
-    pads(("ttb", 0), ("ttb", 112))
     for i, q, st, c in ((7, 0, 8, LOW), (7, 1, 8, 352), (7, 2, 8, 352), (7, 3, 8, -352), (7, 5, 8, -352),
                         (8, 0, 16, LOW), (8, 4, 16, DRAWN), (8, 8, 16, -352), (8, 15, 16, LOW)):
-        act(tab(i, q, st), R("tbs", 224, 224 + 32 // st), bias=float(c))
-    pads(("tf", 0), ("gl", 0), ("gl", 368), ("wa", 0), ("wa", 368), ("wb", 0), ("wb", 368), ("gb", 0), ("gb", 368))
-    tr(R("tc", 0, 64), tab(0, 0, 1, 64))
+        act(tab(i, q, st), R("tbs", 0, 32 // st), bias=float(c))
+    pads(("gl", 0), ("gl", 368), ("tf", 0), ("wb", 0), ("wb", 368))
+    tr(R("tc", 32, 64), tab(1))
     for q, st, c in ((2, 16, 0), (5, 16, 0), (10, 16, 16), (13, 16, 16), (4, 4, 3), (4, 16, 2)):
         ms(tab(2, q, st), float(c))
-    ts(R("offi", 0, 22, 2), R("i2", 0, 22, 2), EVEN, AO.add)
-    ts(R("offi", 1, 22, 2), R("i2", 1, 22, 2), ODD, AO.add)
+    ts(R("offi", 0, 22), R("i2", 0, 22), ROW, AO.add)
     tr(R("tc", 64, 160), tab(2, 0, 1, 96))
     tr(R("tc", 160, 320), tab(5, 0, 1, 160))
 
@@ -259,6 +262,8 @@ def rank_program(g, core, T, topo):
     iota(R("so", 0, F, 4), [[16, 22], [0, 2]], 0)
     iota(R("gam", 0, 24), [[32, 12], [0, 2]], -16 - MID)
     iota(R("gam", 24, 46), [[32, 11], [0, 2]], -MID)
+    for n, a in (("gb", 0), ("gb", 368), ("wa", 0), ("wa", 368), ("mf", 0), ("mo", 368), ("ww", 0)):
+        iota(R(n, a, a + 16), [[0, 16]], 0)
     iota(R("sp", 0, 384), [[0, 384]], 2 * LOW)
     iota(R("wr", 2 * C, 3 * C), [[0, C]], 0)
     one, e = R("ones", 0, 516), R("eb", 0, 516)
@@ -272,18 +277,11 @@ def rank_program(g, core, T, topo):
     ts(R("upk", 0, 8, 2), R("i2", 24, 32, 2), UCOL, AO.add)
     ts(R("upk", 1, 8, 2), R("i2", 25, 32, 2), PAIR, AO.add, UCOL, AO.add)
 
-    ts(R("tbs", 0, 66), R("tbi", 0, 66), float(-MID), AO.add)
-    copy(R("opi", 0, 22), R("tbi", 0, 22))
-    tr(R("ttb", 16, 112), R("tbs", 0, 96))
     ts(PP, UN, 16.0, AO.mult, float(QP), AO.add)
-    tr(R("tbs", 96, 224), R("ttb", 0, 128))
     ts(PD, UN, 16.0, AO.mult, float(QD), AO.add)
-    both("tf", 16, R("tbs", 0, 256), "offi", 10)
-    qm(R("qu", 0, 128), R("su", 0, 128), R("ut", 0, 512))
-    tr(R("wa", 16, 368), R("tf", 16, 368))
-    act(R("sd", 0, 128), R("su", 0, 128), UP)
-    emit("v", lambda: V.tensor_copy(T.qd[:, 0:128].bitcast(dt.uint32), T.qu[:, 0:128].bitcast(dt.uint32).indirect(ap(UP))),
-         [R("qu", 0, 128), UP], [R("qd", 0, 128)])
+    copy(R("opi", 0, 22), R("tbi", 0, 22))
+    ts(R("wa", 16, 176), RAW, float(-MID), AO.add, off=R("offi", 0, 10))
+    act(R("wa", 176, 368), RAW, R("offi", 10, 22), bias=float(-MID))
     LK = R("wa", 16, 368)
     GAB = R("gab", 0, 46)
 
@@ -301,8 +299,8 @@ def rank_program(g, core, T, topo):
     rest = [
         lambda: ts(R("opm", 0, 22), R("tf", 16 + QP, 368, 16), float(MID), AO.add),
         lambda: ts(R("cf", 6, 8), R("i2", 24, 26), 8.0, AO.mult, FIRST, AO.add),
-        lambda: ms(R("cf", 9, 10), float(MID)),
         lambda: ts(P1, R("cf", 6, 8), 175.0, AO.min),
+        lambda: ms(R("cf", 9, 10), float(MID)),
         lambda: ts(GAB, R("gam", 0, 46), P32, AO.add),
         lambda: ts(P2, UN, 4.0, AO.mult, 3.0, AO.add),
         lambda: ts(PK, UN, 16.0, AO.mult, float(QK), AO.add),
@@ -313,8 +311,8 @@ def rank_program(g, core, T, topo):
         lambda: ts(P3, P1, 2.0, AO.mult),
         lambda: ts(PP3, UN3, float(QP), AO.add),
         lambda: ts(PD3, UN3, float(QD), AO.add),
-        lambda: copy(R("sp", 1, C, 16), R("tbs", 0, 22)),
-        lambda: copy(R("sp", 9, C, 16), R("tbs", 0, 22)),
+        lambda: ts(R("sp", 1, C, 16), R("tbi", 0, 22), float(-MID), AO.add),
+        lambda: ts(R("sp", 9, C, 16), R("tbi", 0, 22), float(-MID), AO.add),
     ]
 
     def fill(n):
@@ -342,22 +340,28 @@ def rank_program(g, core, T, topo):
         act(R("xp", C * t + lo, C * t + hi), R("x%d" % r, 4 * lo + t, 4 * hi, 4), scale=0.5)
 
     both("gl", 16, LK, "opi", 8)
-    state_half(0, 1)
-    act(run(4), LK)
-    act(R("wb", 736, 1088), LK)
-    turn("glt", "gl", 0, C)
-    fill(1)
+    qm(R("qu", 0, 128), R("su", 0, 128), R("ut", 0, 512))
+    turn("glt", "gl", 0, 128)
+    turn("glt", "gl", 128, C)
+    tr(R("tc", 320, 480), tab(10, 0, 1, 160))
     pick("td", 64, "glt", R("pk", 2, 6))
+    act(R("sd", 0, 128), R("su", 0, 128), UP)
+    emit("v", lambda: V.tensor_copy(T.qd[:, 0:128].bitcast(dt.uint32), T.qu[:, 0:128].bitcast(dt.uint32).indirect(ap(UP))),
+         [R("qu", 0, 128), UP], [R("qd", 0, 128)])
+    act(run(2), LK, R("td", 0, 22))
+    tr(R("tf", 16, 368), LK)
+    state_half(0, 1)
     state_half(0, 0)
     signs_mm(1)
     signs_mm(0)
-    act(run(2), LK, R("td", 0, 22))
-    tr(R("tc", 320, 480), tab(10, 0, 1, 160))
-    signs_ts(1)
     act(run(0), LK, R("td", 32, 54))
+    act(run(4), LK)
+    fill(2)
+    tr(run(6), R("tf", 14, 366))
+    signs_ts(1)
     fill(1)
     signs_ts(0)
-    fill(2)
+    fill(1)
 
     ALL, TURNED = R("ww", 16, 16 + 5 * C), R("wr", 0, 5 * C)
     ALLB = R("wb", 16, 1088)
@@ -375,20 +379,21 @@ def rank_program(g, core, T, topo):
         arrive(R("sin%d" % r, 0, F), "as%d" % r, n_all)
         X, XN = "x%d" % r, "x%d" % (r + 1)
 
-        k = 14 if r == 0 else 10
+        k = 10
         a = 16 * k
         ts(R("gm", 0, a), BT, KEEP, AO.mult, START, AO.add, off=R("opm", 0, k))
         act(R("gm", a, C), BT, R("opm", k, 22), scale=KEEP, bias=START)
-        if r == 0:
-            tr(run(6), R("tf", 14, 366))
         for t in range(3 if r else 0):
             plane(r, 1, t)
         tr(R("g1", 0, a), R("gm", 0, a))
         tr(R("g1", a, C), R("gm", a, C))
-        fill(1)
+        if r:
+            scan(R("s3", 0, a), R("g1", 0, a), R("sp", 0, a))
+        else:
+            fill(1)
         scan(R("s1", 0, F), R("g1", 0, C, 2), R("so", 0, F))
         if r:
-            scan(R("s3", 0, C), R("g1", 0, C), R("sp", 0, C))
+            scan(R("s3", a, C), R("g1", a, C), R("sp", a, C))
         fill(1)
         ts(R("o1", 0, 32), R("s1", 0, F), Q16, AO.add, 3.0 * C, AO.add, off=P1)
         if r:
@@ -396,7 +401,7 @@ def rank_program(g, core, T, topo):
         fill(1)
         tt(R("wb", 16, 368), ALL, BT, AO.add, off=R("o1", 0, 22))
         if r == 0:
-            pads(("mf", 0), ("mo", 368), ("ww", 0))
+            act(R("wb", 736, 1088), run(4))
             for t in range(4):
                 plane(0, 1, t)
             fill(1)
@@ -420,10 +425,10 @@ def rank_program(g, core, T, topo):
             plane(r, 1, 3)
         turn("gt", "gb", 0, a)
         turn("gt", "gb", a, C)
-        fill(1)
-        copy(R("gt", 3, 736, 16), GAB)
-        fill(1)
-        scan(R("s2", 0, 184), R("gt", 0, 736, 4), R("gt", 3, 736, 4))
+        copy(R("gt", 387, 736, 16), R("gab", 24, 46))
+        copy(R("gt", 3, 384, 16), R("gab", 0, 24))
+        scan(R("s2", 96, 184), R("gt", 384, 736, 4), R("gt", 387, 736, 4))
+        scan(R("s2", 0, 96), R("gt", 0, 384, 4), R("gt", 3, 384, 4))
         fill(1)
         ts(R("o2", 0, 32), R("s2", 0, 184), float(MID), AO.add, off=P2)
         fill(1)
@@ -434,7 +439,8 @@ def rank_program(g, core, T, topo):
         turn("n2", "wa", a, C)
         fill(1)
         OP = "opn%d" % r
-        pick(OP, 64, "n2", R("pk", 4, 8))
+        pick(OP, 32, "n2", PP)
+        ts(R(OP, 32, 64), R("n2", 0, 736), float(MID), AO.add, off=PK)
         KS = R("ks%d" % r, 0, 22)
         send(source, PIN, R(OP, 0, 12), "ap%d" % r)
 
@@ -485,6 +491,7 @@ def rank_program(g, core, T, topo):
         if r == 0:
             turn("glt", "mf", 0, 192)
             evict(1, 0, "v")
+        fill(9)
         pick("om", 16, "glt", PK1)
         if r:
             evict(1, 0, "v")
@@ -508,7 +515,7 @@ def rank_program(g, core, T, topo):
         tr(R("kr", 0, C), R("n1", 384, 736))
         act(R("mo", 176, 368), R("kr", 0, C), R(OP, 10, 22))
         if not last:
-            act(R("n2", 384 + 1, 736, 16), R("n2", 384 + QP, 736, 16))
+            act(R("n2", 384 + QD - 6, 736, 16), R("n2", 384 + QD, 736, 16))
             act(R("n2", 384 + 3, 736, 16), R("n2", 384 + QK, 736, 16))
             turn("glt", "gl", 0, C)
             pick("td", 64, "glt", R("pk", 2, 6))

from concourse.mybir import dt, AluOpType as AO, ActivationFunctionType as AF

C, F = 352, 176
STEP = [2, 4, 1]
MID = 176
ROT, DRAWN = 368, 720
QP, QK, QD = 7, 9, 11
LOW = -4096
TINY = 2.0 ** -40
B16, F32, I32, U16, U8, MXC = "bfloat16", "float32", "int32", "uint16", "uint8", "float8_e4m3fn_x4"

SCRATCH = {
    "tbi": ("sbuf", [128, 24], I32), "raw": ("sbuf", [128, C], I32), "tbs": ("sbuf", [128, 16], B16), "tf": ("sbuf", [128, 384], B16),
    "ones": ("sbuf", [128, 516], B16), "eb": ("sbuf", [128, 516], B16), "qe": ("sbuf", [128, 512], MXC), "se": ("sbuf", [128, 512], U8),
    "cf": ("sbuf", [128, 16], F32), "tb": ("sbuf", [128, 488], F32), "tc": ("sbuf", [128, 480], F32),
    "i2": ("sbuf", [128, 40], F32), "gam": ("sbuf", [128, 48], F32), "gab": ("sbuf", [128, 48], B16),
    "offi": ("sbuf", [128, 24], U16), "pk": ("sbuf", [128, 24], U16), "upk": ("sbuf", [128, 8], U16),
    "wq": ("sbuf", [128, 512], MXC), "wp": ("sbuf", [128, 512], U8),
    "ut": ("sbuf", [128, 512], B16), "qu": ("sbuf", [128, 128], MXC), "su": ("sbuf", [128, 128], U8),
    "qd": ("sbuf", [128, 128], MXC), "sd": ("sbuf", [128, 128], U8),
    "vt": ("sbuf", [128, 512], B16), "qv": ("sbuf", [128, 128], MXC), "sv": ("sbuf", [128, 128], U8),
    "x0": ("sbuf", [128, 4 * C], B16), "x1": ("sbuf", [128, 4 * C], B16), "x2": ("sbuf", [128, 4 * C], B16), "x3": ("sbuf", [128, 4 * C], B16),
    "xp": ("sbuf", [128, 4 * C], B16), "hp": ("sbuf", [128, 4 * C], B16), "zp": ("sbuf", [128, 4 * C], B16), "zt": ("sbuf", [128, 4 * C], B16),
    "ft": ("sbuf", [128, 4 * F], B16),
    "qx": ("sbuf", [128, C], MXC), "sx": ("sbuf", [128, C], U8), "qz": ("sbuf", [128, C], MXC), "sz": ("sbuf", [128, C], U8),
    "bt": ("sbuf", [128, C], B16), "ww": ("sbuf", [128, 1776], B16), "wr": ("sbuf", [128, 1760], B16), "td": ("sbuf", [128, 64], U16),
    "wa": ("sbuf", [128, 384], B16), "wb": ("sbuf", [128, 1088], B16),
    "gm": ("sbuf", [128, C], B16), "g1": ("sbuf", [128, C], B16), "so": ("sbuf", [128, F], B16), "s1": ("sbuf", [128, F], B16),
    "sp": ("sbuf", [128, 384], B16), "s3": ("sbuf", [128, C], B16),
    "gb": ("sbuf", [128, 384], B16), "gl": ("sbuf", [128, 384], B16), "mf": ("sbuf", [128, 384], B16), "mo": ("sbuf", [128, 384], B16),
    "gt": ("sbuf", [128, 752], B16), "glt": ("sbuf", [128, 752], B16), "n1": ("sbuf", [128, 752], B16), "n2": ("sbuf", [128, 752], B16),
    "mt": ("sbuf", [128, 752], B16), "kr": ("sbuf", [128, C], B16), "s2": ("sbuf", [128, 184], F32),
    "o1": ("sbuf", [128, 32], U16), "o2": ("sbuf", [128, 32], U16), "op1": ("sbuf", [128, 32], U16),
    "opi": ("sbuf", [128, 32], U16), "opm": ("sbuf", [128, 32], U16), "om": ("sbuf", [128, 16], U16), "oo": ("sbuf", [128, 16], U16),
    "lkt": ("sbuf", [128, C], F32), "yt": ("sbuf", [128, C], F32),
    "ps": ("psum", [128, 4096], F32),
}
for _r in range(3):
    SCRATCH["opn%d" % _r] = ("sbuf", [128, 64], U16)
    SCRATCH["ks%d" % _r] = ("sbuf", [128, 22], B16)
    SCRATCH["pin%d" % _r] = ("sbuf", [128, 22], U16)
    SCRATCH["kin%d" % _r] = ("sbuf", [128, 22], B16)
    SCRATCH["qf%d" % _r] = ("sbuf", [128, F], MXC)
    SCRATCH["sf%d" % _r] = ("sbuf", [128, F], U8)
    SCRATCH["qin%d" % _r] = ("sbuf", [128, F], MXC)
    SCRATCH["sin%d" % _r] = ("sbuf", [128, F], U8)
SEMAPHORES = ["cv", "cs", "ct", "cg", "sent", "sty", "sta",
              "ldp", "lda", "ldb", "ldx", "ldu", "ldv", "ldwc", "ldws"]
SEMAPHORES += [k + str(r) for r in range(3) for k in ("ap", "ak", "ac", "as")]


def make_tracker(g, T):
    queues = {"v": g.vector, "s": g.scalar, "t": g.tensor, "g": g, "y": g.sync}
    own = {"v": "cv", "s": "cs", "t": "ct", "g": "cg"}
    count = {}
    known = {q: {} for q in queues}
    snaps = {}
    hist = {}

    def span(r):
        n, lo, hi, st = r
        return (n, lo // 512 * 512, (hi + 511) // 512 * 512, 1) if n == "ps" else r

    def meet(a, b):
        if a[1] >= b[2] or b[1] >= a[2]:
            return False
        st = min(a[3], b[3])
        return not (st > 1 and a[3] % st == 0 and b[3] % st == 0 and (a[1] - b[1]) % st)

    def note(r, write, tok):
        r = span(r)
        h = hist.setdefault(r[0], [])
        if r[3] == 0:
            r = r[:3] + (1,)
        elif write and r[3] == 1:
            h[:] = [e for e in h if not (r[1] <= e[0][1] and e[0][2] <= r[2])]
        h.append((r, write, tok))

    def wait(q, need):
        for sem in sorted(need):
            val = need[sem]
            if known[q].get(sem, 0) >= val:
                continue
            if any(o != sem and known[q].get(o, 0) < need[o] and snaps.get((o, need[o]), {}).get(sem, 0) >= val for o in need):
                continue
            queues[q].wait_ge(T.sem[sem], val)
        for sem in need:
            known[q][sem] = max(known[q].get(sem, 0), need[sem])
            for s, v in snaps.get((sem, need[sem]), {}).items():
                known[q][s] = max(known[q].get(s, 0), v)

    def deps(reads, writes):
        need = {}
        for rs, w in ((reads, False), (writes, True)):
            for r in rs:
                r = span(r)
                for e, ew, tok in hist.get(r[0], []):
                    if (w or ew) and meet(r, e):
                        need[tok[0]] = max(need.get(tok[0], 0), tok[1])
        return need

    def emit(q, call, reads, writes, sem=None, inc=1):
        wait(q, deps(reads, writes))
        name = sem or own[q]
        call().then_inc(T.sem[name], inc)
        count[name] = count.get(name, 0) + inc
        tok = (name, count[name])
        snaps[tok] = dict(known[q])
        for r in reads:
            note(r, False, tok)
        for r in writes:
            note(r, True, tok)

    def arrive(r, sem, val):
        note(r, True, (sem, val))

    def ready(q, reads):
        wait(q, deps(reads, []))

    return emit, arrive, ready, count


def rank_program(g, core, T, topo):
    rank = T.rank_of(core)
    if rank is None:
        return
    emit, arrive, ready, count = make_tracker(g, T)
    V, S, PE = g.vector, g.scalar, g.tensor

    def R(n, lo, hi, st=1):
        return (n, lo, hi, st)

    def ap(r):
        return T[r[0]][:, r[1]:r[2]] if r[3] == 1 else T[r[0]][:, r[1]:r[2]:r[3]]

    def src(r, off):
        return ap(r) if off is None else ap(r).indirect(ap(off))

    def rd(*rs):
        return [r for r in rs if isinstance(r, tuple)]

    def val(x):
        return ap(x) if isinstance(x, tuple) else x

    def copy(out, in_, off=None):
        emit("v", lambda: V.tensor_copy(ap(out), src(in_, off)), rd(in_, off), [out])

    def ts(out, in_, s1, op0, s2=None, op1=None, off=None):
        if op1 is None:
            emit("v", lambda: V.tensor_scalar(ap(out), src(in_, off), val(s1), None, op0), rd(in_, off, s1), [out])
        else:
            emit("v", lambda: V.tensor_scalar(ap(out), src(in_, off), val(s1), val(s2), op0, op1), rd(in_, off, s1, s2), [out])

    def tt(out, a, b, op, off=None):
        emit("v", lambda: V.tensor_tensor(ap(out), src(a, off), ap(b), op), rd(a, b, off), [out])

    def scan(out, a, b):
        emit("v", lambda: V.tensor_tensor_scan(ap(out), ap(a), ap(b), 0.0, AO.add, AO.max), [a, b], [out])

    def tr(out, in_):
        emit("v", lambda: V.transpose(ap(out), ap(in_)), [in_], [out])

    def ms(out, c):
        emit("v", lambda: V.memset(ap(out), c), [], [out])

    def qm(q, s, in_):
        emit("v", lambda: V.quantize_mx(ap(q), ap(s), ap(in_)), [in_], [q, s])

    def act(out, in_, off=None, scale=1.0, bias=None):
        if bias is not None:
            emit("s", lambda: S.activation(ap(out), src(in_, off), AF.Identity, bias=val(bias), scale=val(scale)), rd(in_, off, bias, scale), [out])
            return
        if scale == 1.0:
            emit("s", lambda: S.activation(ap(out), src(in_, off), AF.Copy), rd(in_, off), [out])
            return
        func = AF.Identity if isinstance(scale, tuple) else AF.Copy
        emit("s", lambda: S.activation(ap(out), src(in_, off), func, scale=val(scale)), rd(in_, off, scale), [out])

    def both(out, lo, win, off, k, n=22):
        copy(R(out, lo, lo + 16 * k), win, R(off, 0, k))
        act(R(out, lo + 16 * k, lo + 16 * n), win, R(off, k, n))

    def mm(bank, n, w, ws, x, xs):
        out = R("ps", 512 * bank, 512 * bank + n)
        emit("t", lambda: PE.matmul_mx(ap(out), ap(w), ap(ws), ap(x), ap(xs), True, True), [w, ws, x, xs], [out])
        return out

    def load(q, out, in_ap, sem, code=False):
        eng = {"y": g.sync, "s": g.scalar}[q]
        emit(q, lambda: eng.dma_start(ap(out).bitcast(dt.uint8) if code else ap(out), in_ap), [], [out], sem, 16)

    def iota(out, pattern, base):
        emit("g", lambda: g.iota(ap(out), pattern, base, 0, allow_small_or_imprecise_dtypes=True), [], [out])

    def send(d, ds, sr, sem, code=False):
        ready("g", [sr])
        rid, pid = topo.addr(d, core)
        a, b = (ap(ds).bitcast(dt.uint8), ap(sr).bitcast(dt.uint8)) if code else (ap(ds), ap(sr))
        g.remote_dma(a, b, T.sem[sem], T.sem["sent"], pid, rid, topo.mask(core, d))
        count["sent"] = count.get("sent", 0) + len(topo.engines(core, d))

    RAW = R("raw", 0, C)
    emit("v", lambda: V.memset(ap(RAW), MID), [], [RAW])
    load("s", R("tbi", 0, 22), T.pl[:], "ldp")
    for q, eng, sem, rows in (("s", S, "lda", ((QP, T.pl), (QD, T.dl))), ("y", g.sync, "ldb", ((QK, T.kl), (QD - 6, T.dl), (QK - 6, T.kl)))):
        ready(q, [RAW])
        for c, t in rows:
            eng.dma_start(T.raw[c:128:16, :], t[:]).then_inc(T.sem[sem], 16)
    arrive(RAW, "lda", 32)
    arrive(R("raw", 0, C, 0), "ldb", 48)
    load("s", R("ut", 0, 512), T.u[:], "ldu")
    load("y", R("x0", 0, 4 * C), T.x[:], "ldx")
    ready("y", [R("x0", 0, 4 * C)])
    load("y", R("wq", 0, 512), T.wc[:], "ldwc", True)
    load("y", R("wp", 0, 512), T.ws[:], "ldws")
    load("y", R("vt", 0, 512), T.v[:], "ldv")

    def tab(i, q=0, st=1, n=32):
        return R("tb", 32 * i + q, 32 * i + n, st)

    (ROW, UCOL, PAIR, UNIT, WT, KEEP, START, NB, RM, Q16, P32, FIRST, UPPER, TWICE) = [R("tc", 32 * i, 32 * i + 1) for i in range(1, 15)]
    zero = R("tbs", 0, 16)
    ms(zero, 0.0)
    iota(tab(1), [[0, 2], [22, 16]], 0)
    iota(R("i2", 0, 22), [[1, 22]], 0)
    iota(tab(2), [[0, 2], [16, 2], [0, 8]], 1)
    iota(R("i2", 24, 32), [[16, 8]], 0)
    ms(tab(3), -16.0)
    ms(tab(5, 0, 1, 160), 0.0)
    ms(tab(3, 0, 4), 0.0)
    for i, a, b, c, d in ((4, [[2, 8], [-22, 2]], 24, [[2, 8], [24, 2]], 1), (13, [[2, 8], [24, 2]], 12, [[2, 8], [-22, 2]], 35),
                          (14, [[2, 4], [-22, 2], [0, 2]], 24, [[2, 4], [24, 2], [0, 2]], 1)):
        iota(tab(i, 0, 1, 16), a, b)
        iota(tab(i, 16), c, d)
    iota(tab(10), [[0, 2], [1, 16]], 0)
    iota(tab(11), [[1, 32]], 0)
    iota(tab(12), [[4, 2], [8, 16]], 3)
    for i, q, st, c in ((5, 1, 8, -704 * TINY), (5, 2, 8, -1056), (5, 3, 8, 704 * TINY), (5, 5, 8, 352 * TINY), (5, 6, 8, -352),
                        (5, 4, 16, LOW), (5, 8, 16, 704), (5, 12, 16, -352), (6, 2, 4, 1), (6, 1, 2, 1 / TINY), (9, 1, 2, 1)):
        ms(tab(i, q, st), float(c))

    def pads(*where):
        for n, a in where:
            act(R(n, a, a + 16), zero)
    for i, q, st, c in ((7, 0, 8, LOW), (7, 1, 8, 352), (7, 2, 8, 352), (7, 3, 8, -352), (7, 5, 8, -352),
                        (8, 0, 16, LOW), (8, 4, 16, DRAWN), (8, 8, 16, -352), (8, 15, 16, LOW)):
        act(tab(i, q, st), R("tbs", 0, 32 // st), bias=float(c))
    pads(("gl", 0), ("gl", 368), ("tf", 0), ("wb", 0), ("wb", 368))
    tr(R("tc", 32, 64), tab(1))
    for q, st, c in ((2, 16, 0), (5, 16, 0), (10, 16, 16), (13, 16, 16), (4, 4, 3), (4, 16, 2)):
        ms(tab(2, q, st), float(c))
    ts(R("offi", 0, 22), R("i2", 0, 22), ROW, AO.add)
    tr(R("tc", 64, 160), tab(2, 0, 1, 96))
    tr(R("tc", 160, 320), tab(5, 0, 1, 160))

    def run(i):
        a = C * (0, 1, 3, 4)[i // 2]
        return R("wr", a, a + C) if i % 2 else R("ww", 16 + a, 16 + a + C)

    iota(R("so", 0, F), [[0, F]], 2 * LOW)
    iota(R("ww", 16 + 2 * C, 16 + 3 * C), [[0, C]], 0)
    iota(R("so", 0, F, 4), [[16, 22], [0, 2]], 0)
    iota(R("gam", 0, 24), [[32, 12], [0, 2]], -16 - MID)
    iota(R("gam", 24, 46), [[32, 11], [0, 2]], -MID)
    for n, a in (("gb", 0), ("gb", 368), ("wa", 0), ("wa", 368), ("mf", 0), ("mo", 368), ("ww", 0)):
        iota(R(n, a, a + 16), [[0, 16]], 0)
    iota(R("sp", 0, 384), [[0, 384]], 2 * LOW)
    iota(R("wr", 2 * C, 3 * C), [[0, C]], 0)
    one, e = R("ones", 0, 516), R("eb", 0, 516)
    iota(one, [[0, 516]], 1)
    emit("g", lambda: g.affine_select(ap(e), ap(one), [[-1, 516]], AO.is_equal, 0.0, 3, 4), [one], [e])

    P1, PD, PP, PK, PK1, PO, P2 = R("pk", 0, 2), R("pk", 2, 4), R("pk", 4, 6), R("pk", 6, 8), R("pk", 6, 7), R("pk", 8, 9), R("pk", 10, 12)
    P3, PP3, PD3 = R("pk", 22, 24), R("pk", 14, 17), R("pk", 18, 21)
    UN, UN3, UP = R("cf", 0, 2), R("cf", 2, 5), R("upk", 0, 8)
    ts(UN, R("i2", 24, 26), UNIT, AO.add, 45.0, AO.min)
    ts(R("upk", 0, 8, 2), R("i2", 24, 32, 2), UCOL, AO.add)
    ts(R("upk", 1, 8, 2), R("i2", 25, 32, 2), PAIR, AO.add, UCOL, AO.add)

    ts(PP, UN, 16.0, AO.mult, float(QP), AO.add)
    ts(PD, UN, 16.0, AO.mult, float(QD), AO.add)
    copy(R("opi", 0, 22), R("tbi", 0, 22))
    ts(R("wa", 16, 176), RAW, float(-MID), AO.add, off=R("offi", 0, 10))
    act(R("wa", 176, 368), RAW, R("offi", 10, 22), bias=float(-MID))
    LK = R("wa", 16, 368)
    GAB = R("gab", 0, 46)

    def turn(dst, srcb, a, b, at=0):
        tr(R(dst, 384 + a, 384 + b), R(srcb, at + 16 + a, at + 16 + b))
        e = 384 if b == C else b
        tr(R(dst, a, e), R(srcb, at + a, at + e))

    def pick(out, n, units, lst):
        ts(R(out, 0, n), R(units, 0, 736), float(MID), AO.add, off=lst)

    def unpacker(b):
        qm(R("qe", 128 * b, 128 * b + 128), R("se", 128 * b, 128 * b + 128), R("eb", 3 - b, 515 - b))

    rest = [
        lambda: ts(R("opm", 0, 22), R("tf", 16 + QP, 368, 16), float(MID), AO.add),
        lambda: ts(R("cf", 6, 8), R("i2", 24, 26), 8.0, AO.mult, FIRST, AO.add),
        lambda: ts(P1, R("cf", 6, 8), 175.0, AO.min),
        lambda: ms(R("cf", 9, 10), float(MID)),
        lambda: ts(GAB, R("gam", 0, 46), P32, AO.add),
        lambda: ts(P2, UN, 4.0, AO.mult, 3.0, AO.add),
        lambda: ts(PK, UN, 16.0, AO.mult, float(QK), AO.add),
        lambda: ts(R("cf", 8, 9), UPPER, 45.0, AO.min),
        lambda: ts(R("cf", 10, 13), R("i2", 24, 27), 0.5, AO.mult, TWICE, AO.add),
        lambda: ts(PO, R("cf", 8, 9), 16.0, AO.mult, float(QK), AO.add),
        lambda: ts(UN3, R("cf", 10, 13), 45.0, AO.min, 16.0, AO.mult),
        lambda: ts(P3, P1, 2.0, AO.mult),
        lambda: ts(PP3, UN3, float(QP), AO.add),
        lambda: ts(PD3, UN3, float(QD), AO.add),
        lambda: ts(R("sp", 1, C, 16), R("tbi", 0, 22), float(-MID), AO.add),
        lambda: ts(R("sp", 9, C, 16), R("tbi", 0, 22), float(-MID), AO.add),
    ]

    def fill(n):
        for i in range(n):
            if rest:
                rest.pop(0)()

    def half(h):
        return (0, F) if h == 0 else (F, C)

    def state_half(r, h):
        lo, hi = half(h)
        qm(R("qx", lo, hi), R("sx", lo, hi), R("x%d" % r, 4 * lo, 4 * hi))

    def signs_mm(h):
        lo, hi = half(h)
        mm(5 - h, F, R("qd", 0, 128), R("sd", 0, 128), R("qx", lo, hi), R("sx", lo, hi))

    def signs_ts(h):
        lo, hi = half(h)
        ts(R("bt", lo, hi), R("ps", 512 * (5 - h), 512 * (5 - h) + F), 0.0, AO.is_gt, WT, AO.mult)

    def plane(r, h, t):
        lo, hi = half(h)
        act(R("xp", C * t + lo, C * t + hi), R("x%d" % r, 4 * lo + t, 4 * hi, 4), scale=0.5)

    both("gl", 16, LK, "opi", 8)
    qm(R("qu", 0, 128), R("su", 0, 128), R("ut", 0, 512))
    turn("glt", "gl", 0, 128)
    turn("glt", "gl", 128, C)
    tr(R("tc", 320, 480), tab(10, 0, 1, 160))
    pick("td", 64, "glt", R("pk", 2, 6))
    act(R("sd", 0, 128), R("su", 0, 128), UP)
    emit("v", lambda: V.tensor_copy(T.qd[:, 0:128].bitcast(dt.uint32), T.qu[:, 0:128].bitcast(dt.uint32).indirect(ap(UP))),
         [R("qu", 0, 128), UP], [R("qd", 0, 128)])
    act(run(2), LK, R("td", 0, 22))
    tr(R("tf", 16, 368), LK)
    state_half(0, 1)
    state_half(0, 0)
    signs_mm(1)
    signs_mm(0)
    act(run(0), LK, R("td", 32, 54))
    act(run(4), LK)
    fill(2)
    tr(run(6), R("tf", 14, 366))
    signs_ts(1)
    fill(1)
    signs_ts(0)
    fill(1)

    ALL, TURNED = R("ww", 16, 16 + 5 * C), R("wr", 0, 5 * C)
    ALLB = R("wb", 16, 1088)
    BT = R("bt", 0, C)

    for r in range(3):
        s = STEP[r]
        source, target = T.cores[(rank - s) % 8], T.cores[(rank + s) % 8]
        last = r == 2
        n_all = len(topo.engines(core, target))
        PIN = R("pin%d" % r, 0, 12)
        arrive(PIN, "ap%d" % r, len(topo.engines(source, core)))
        arrive(R("kin%d" % r, 0, 22), "ak%d" % r, n_all)
        arrive(R("qin%d" % r, 0, F), "ac%d" % r, n_all)
        arrive(R("sin%d" % r, 0, F), "as%d" % r, n_all)
        X, XN = "x%d" % r, "x%d" % (r + 1)

        k = 10
        a = 16 * k
        ts(R("gm", 0, a), BT, KEEP, AO.mult, START, AO.add, off=R("opm", 0, k))
        act(R("gm", a, C), BT, R("opm", k, 22), scale=KEEP, bias=START)
        for t in range(3 if r else 0):
            plane(r, 1, t)
        tr(R("g1", 0, a), R("gm", 0, a))
        tr(R("g1", a, C), R("gm", a, C))
        if r:
            scan(R("s3", 0, a), R("g1", 0, a), R("sp", 0, a))
        else:
            fill(1)
        scan(R("s1", 0, F), R("g1", 0, C, 2), R("so", 0, F))
        if r:
            scan(R("s3", a, C), R("g1", a, C), R("sp", a, C))
        fill(1)
        ts(R("o1", 0, 32), R("s1", 0, F), Q16, AO.add, 3.0 * C, AO.add, off=P1)
        if r:
            ts(R("op1", 0, 32), R("s3", 0, C), float(MID), AO.add, off=P3)
        fill(1)
        tt(R("wb", 16, 368), ALL, BT, AO.add, off=R("o1", 0, 22))
        if r == 0:
            act(R("wb", 736, 1088), run(4))
            for t in range(4):
                plane(0, 1, t)
            fill(1)
            turn("n1", "wb", 0, C)
            fill(1)
            pick("op1", 32, "n1", PP)
            fill(1)
        else:
            act(R("wb", 384, 736), TURNED, R("o1", 0, 22))

        k = 8
        a = 16 * k
        CB = R("wb", 16, 368)
        act(R("gb", 16 + a, 368), CB, R("op1", k, 22), bias=NB)
        ts(R("gb", 16, 16 + a), CB, NB, AO.add, off=R("op1", 0, k))
        if r == 0:
            tr(R("wb", 384, 736), R("n1", 382, 734))
            for t in range(4):
                plane(0, 0, t)
        else:
            plane(r, 1, 3)
        turn("gt", "gb", 0, a)
        turn("gt", "gb", a, C)
        copy(R("gt", 387, 736, 16), R("gab", 24, 46))
        copy(R("gt", 3, 384, 16), R("gab", 0, 24))
        scan(R("s2", 96, 184), R("gt", 384, 736, 4), R("gt", 387, 736, 4))
        scan(R("s2", 0, 96), R("gt", 0, 384, 4), R("gt", 3, 384, 4))
        fill(1)
        ts(R("o2", 0, 32), R("s2", 0, 184), float(MID), AO.add, off=P2)
        fill(1)
        act(R("wa", 16 + a, 368), ALLB, R("o2", k, 22), scale=RM)
        ts(R("wa", 16, 16 + a), ALLB, RM, AO.mult, off=R("o2", 0, k))
        fill(1)
        turn("n2", "wa", 0, a)
        turn("n2", "wa", a, C)
        fill(1)
        OP = "opn%d" % r
        pick(OP, 32, "n2", PP)
        ts(R(OP, 32, 64), R("n2", 0, 736), float(MID), AO.add, off=PK)
        KS = R("ks%d" % r, 0, 22)
        send(source, PIN, R(OP, 0, 12), "ap%d" % r)

        RUNS = ((0, 14), (14, 22))
        for c, (k0, k1) in enumerate(RUNS):
            lo, hi = 16 * k0, 16 * k1
            for t, j0, j1 in ([(3, 0, 6), (0, 0, 14), (1, 0, 14), (2, 0, 14), (3, 6, 14)] if c == 0 else [(t, k0, k1) for t in range(4)]):
                win = R("xp", C * t, C * t + C)
                zp = R("zp", C * t + 16 * j0, C * t + 16 * j1)
                (copy if j1 == 6 else act)(zp, win, R(OP, j0, j1))
                tt(R("zt", 64 * j0 + t, 64 * j1, 4), win, zp, AO.add, off=R(OP, 32 + j0, 32 + j1))
            if c == 0:
                copy(KS, R("n2", 384 + QK, 736, 16))
                send(target, R("kin%d" % r, 0, 22), KS, "ak%d" % r)
            elif not last:
                ts(R("opm", 0, 22), R("n2", 384 + QP, 736, 16), float(MID), AO.add)
            qm(R("qz", lo, hi), R("sz", lo, hi), R("zt", 4 * lo, 4 * hi))
            for b in range(4):
                mm(4 * c + b, hi - lo, R("wq", 128 * b, 128 * b + 128), R("wp", 128 * b, 128 * b + 128), R("qz", lo, hi), R("sz", lo, hi))

        def evict(c, b, q):
            lo, hi = 16 * RUNS[c][0], 16 * RUNS[c][1]
            bank = 512 * (4 * c + b)
            out, in_ = R("hp", C * b + lo, C * b + hi), R("ps", bank, bank + hi - lo)
            if q == "s":
                act(out, in_, scale=0.03125)
            else:
                ts(out, in_, 0.03125, AO.mult)

        def part(b, q, j0=0, j1=11):
            ft, hw = R("ft", 64 * j0 + b, 64 * j1, 4), R("hp", C * b, C * b + C)
            if q == "s":
                act(ft, hw, R("om", j0, j1))
            else:
                copy(ft, hw, R("om", j0, j1))

        if r:
            act(R("mf", 16, 208), LK, PIN)
        evict(0, 0, "s")
        evict(0, 1, "s")
        if r:
            turn("glt", "mf", 0, 192)
        else:
            act(R("mf", 16, 208), LK, PIN)
            unpacker(0)
        evict(0, 2, "s")
        evict(0, 3, "v")
        if r == 0:
            turn("glt", "mf", 0, 192)
            evict(1, 0, "v")
        fill(9)
        pick("om", 16, "glt", PK1)
        if r:
            evict(1, 0, "v")
        evict(1, 1, "v")
        part(0, "s")
        evict(1, 2, "v")
        evict(1, 3, "v")
        part(1, "s")
        part(2, "v")
        part(3, "v", 0, 6)
        part(3, "s", 6, 11)
        QF, SF = R("qf%d" % r, 0, F), R("sf%d" % r, 0, F)
        qm(QF, SF, R("ft", 0, 4 * F))

        send(target, R("qin%d" % r, 0, F), QF, "ac%d" % r, True)
        send(target, R("sin%d" % r, 0, F), SF, "as%d" % r)

        act(R("n1", 384 + QK, 736, 16), R("kin%d" % r, 0, 22))
        if not last:
            act(R("gl", 16, 368), LK, R(OP, 0, 22))
        tr(R("kr", 0, C), R("n1", 384, 736))
        act(R("mo", 176, 368), R("kr", 0, C), R(OP, 10, 22))
        if not last:
            act(R("n2", 384 + QD - 6, 736, 16), R("n2", 384 + QD, 736, 16))
            act(R("n2", 384 + 3, 736, 16), R("n2", 384 + QK, 736, 16))
            turn("glt", "gl", 0, C)
            pick("td", 64, "glt", R("pk", 2, 6))
        else:
            qm(R("qv", 0, 128), R("sv", 0, 128), R("vt", 0, 512))
        tr(R("gt", 384 + 160, 736), R("mo", 176, 368))
        tr(R("gt", 192, 384), R("mo", 192, 384))
        if not last:
            tr(run(6), R("n2", 382, 734))
            act(run(2), LK, R("td", 0, 22))
            act(run(0), LK, R("td", 32, 54))
            act(run(3), run(6), R("td", 0, 22))
            act(run(1), run(6), R("td", 32, 54))
            act(R("sp", 0, 384, 8), R("n2", 0, 736), PD3)
        if r == 0:
            unpacker(1)
        pick("oo", 16, "gt", PO)
        if r == 0:
            unpacker(2)
        for t in range(4):
            tt(R(XN, 4 * F + t, 4 * C, 4), R("hp", C * t, C * t + C), R(X, 4 * F + t, 4 * C, 4), AO.add, off=R("oo", 0, 11))
        if r == 0:
            unpacker(3)
        state_half(r + 1, 1)
        if not last:
            turn("mt", "ww", 0, C, C)
            turn("glt", "ww", 0, C)
            if r == 0:
                tr(run(5), R("tf", 14, 366))
            act(R("sp", 3, 384, 8), R("mt", 0, 736), PP3)
            act(R("sp", 2, 384, 8), R("glt", 0, 736), PP3)
        else:
            store(g, T, emit, ap, R, mm, act, ts, 1)
            lkt = R("lkt", 0, C)
            act(lkt, LK, bias=R("cf", 9, 10))
            for i, q in enumerate((QP, QD, QK)):
                emit("y", lambda: g.sync.dma_start(T.lk[:, C * i:C * i + C], T.lkt[q:128:16, :]), [lkt], [], "sty", 16)

        for b in range(4):
            out = mm(b, F, R("qe", 128 * b, 128 * b + 128), R("se", 128 * b, 128 * b + 128), R("qin%d" % r, 0, F), R("sin%d" % r, 0, F))
            tt(R(XN, b, 4 * F, 4), out, R(X, b, 4 * F, 4), AO.add)
            if not last:
                plane(r + 1, 0, b)
        if not last:
            signs_mm(1)
        state_half(r + 1, 0)
        if not last:
            signs_mm(0)
            signs_ts(1)
            tr(run(7), R("n2", 380, 732))
            signs_ts(0)
        else:
            store(g, T, emit, ap, R, mm, act, ts, 0)

    for n in ("cv", "cs", "ct", "cg", "sent", "sty", "sta"):
        if count.get(n):
            g.wait_ge(T.sem[n], count[n])


def store(g, T, emit, ap, R, mm, act, ts, h):
    lo, hi = (0, F) if h == 0 else (F, C)
    Q, P, Y = R("qx", lo, hi), R("sx", lo, hi), R("yt", lo, hi)
    out = mm(5 - h, F, R("qv", 0, 128), R("sv", 0, 128), Q, P)
    emit("y", lambda: g.sync.dma_start(T.oc[:, 4 * lo:4 * hi], ap(Q).bitcast(dt.uint8)), [Q], [], "sty", 16)
    for k in range(4):
        q, e, sem = ("s", g.scalar, "sta") if k % 2 else ("y", g.sync, "sty")
        emit(q, lambda: e.dma_start(T.osc[4 * k:4 * k + 4, lo:hi], T.sx[32 * k:32 * k + 4, lo:hi]), [P], [], sem, 16)
    if h:
        act(Y, out)
    else:
        ts(Y, out, 1.0, AO.mult)
    emit("y", lambda: g.sync.dma_start(T.y[:, lo:hi], ap(Y)), [Y], [], "sty", 16)
